import numpy as np
import ml_dtypes


def mxq(x, axis, fmt="e4m3"):
    dtype, down = {"e4m3": (ml_dtypes.float8_e4m3fn, 7), "e5m2": (ml_dtypes.float8_e5m2, 14)}[fmt]
    v = np.moveaxis(np.asarray(x, np.float32).astype(ml_dtypes.bfloat16).astype(np.float64), axis, -1)
    blocks = v.reshape(v.shape[:-1] + (-1, 32))
    amax = np.abs(blocks).max(-1, keepdims=True)
    byte = np.maximum(np.where(amax > 0, np.frexp(amax)[1] - 1 + 127, 0) - down, 1)
    scale = np.exp2(byte - 127.0)
    codes = (blocks / scale).astype(np.float32).astype(dtype).astype(np.float64)
    return np.moveaxis((codes * scale).reshape(v.shape), -1, axis)


WIDE = False


def mx_kscale(k):
    if not WIDE:
        return np.ones(k)
    levels = np.array([10, -10, 5, -5, 0])
    if k % 512:
        return np.exp2(np.random.permutation(np.resize(levels, k // 32))).repeat(32)
    a = np.empty((k // 512, 16))
    for p in range(k // 512):
        a[p, :8] = np.random.permutation(np.resize(levels, 8))
        for g in range(8):
            far = levels[np.abs(levels - a[p, g]) >= 10]
            a[p, g + 8] = far[np.random.randint(len(far))]
    return np.exp2(a.ravel()).repeat(32)


def f64(x):
    return np.asarray(x).astype(np.float64)


def striped(idx):
    return np.tile(idx.reshape(-1, 16).T, (8, 1)).astype(np.uint16)


def unstriped(offs):
    return offs[:16].T.reshape(-1).astype(np.int64)


E2M1 = np.array([0.0, 0.5, 1.0, 1.5, 2.0, 3.0, 4.0, 6.0, -0.0, -0.5, -1.0, -1.5, -2.0, -3.0, -4.0, -6.0])


def pack_weight(w, fmt):
    k, n = w.shape
    w = f64(np.asarray(w, np.float32).astype(ml_dtypes.bfloat16)).reshape(k // 32, 32, n)
    amax = np.abs(w).max(1)
    if fmt == "e4m3":
        byte = np.frexp(amax)[1] - 1 + 127 - 7
    else:
        mant, ex = np.frexp(amax / 6.0)
        byte = np.where(mant > 0.5, ex, ex - 1) + 127
    byte = np.clip(np.where(amax > 0, byte, 1), 1, 254)
    scaled = (w * np.exp2(127.0 - byte)[:, None, :]).reshape(k, n).astype(np.float32)
    by_word = np.ascontiguousarray(scaled.reshape(k // 512, 128, 4, n).transpose(0, 1, 3, 2))
    if fmt == "e4m3":
        words = by_word.astype(ml_dtypes.float8_e4m3fn).view(np.uint8)
    else:
        c = by_word.astype(ml_dtypes.float4_e2m1fn).view(np.uint8) & 0xF
        words = (c[..., 0::2] | (c[..., 1::2] << 4)).reshape(k // 512, 128, 2 * n)
    return np.ascontiguousarray(words), np.ascontiguousarray(byte.astype(np.uint8).reshape(k // 512, 16, n))


def unpack_weight(words, scales, fmt):
    g, _, n = scales.shape
    words = np.ascontiguousarray(words).reshape(g, 128, n, -1)
    if fmt == "e4m3":
        vals = words.view(ml_dtypes.float8_e4m3fn).astype(np.float64)
    else:
        nib = np.empty((g, 128, n, 4), np.uint8)
        nib[..., 0::2] = words & 0xF
        nib[..., 1::2] = words >> 4
        vals = E2M1[nib]
    vals = vals * np.repeat(np.exp2(scales.astype(np.float64) - 127.0), 8, axis=1)[..., None]
    return vals.transpose(0, 1, 3, 2).reshape(g * 512, n)


def gelu(v):
    return 0.5 * v * (1.0 + np.tanh(np.sqrt(2.0 / np.pi) * (v + 0.044715 * v**3)))


def bf(x):
    return np.asarray(x, np.float32).astype(ml_dtypes.bfloat16)


def planes(Y):
    n, m = Y.shape
    b = f64(bf(Y)).reshape(n // 32, 32, m)
    amax = np.abs(b).max(1)
    byte = np.clip(np.where(amax > 0, np.frexp(amax)[1] - 1 + 127 - 7, 1), 1, 254)
    codes = (b * np.exp2(127.0 - byte)[:, None, :]).reshape(n, m).astype(np.float32).astype(ml_dtypes.float8_e4m3fn).view(np.uint8)
    words = codes.reshape(n // 512, 128, 4, m).transpose(0, 1, 3, 2)
    return np.ascontiguousarray(words), np.ascontiguousarray(byte.astype(np.uint8).reshape(n // 512, 16, m))


K, T, H, S, T2, P, N = 512, 2048, 1024, 1024, 2048, 1024, 512

def setup_inputs():
    n = np.random.standard_normal
    s = mx_kscale(K)[:, None]
    u = mx_kscale(H)[:, None]
    tab_words, tab_scales = pack_weight(n((K, T)) * s, "e4m3")
    w1 = (n((K, H)) / np.sqrt(K) / s * u.T).astype(np.float32)
    w2_words, w2_scales = pack_weight(n((K, H)) / np.sqrt(K) / s, "e2m1")
    w3_words, w3_scales = pack_weight(n((K, H)) / np.sqrt(K) / s, "e4m3")
    page0 = (n((H, T2)) * u).astype(np.float32)
    wgs = np.exp(0.3 * n((128, S))).astype(np.float32)
    w4 = (n((H, N)) * np.exp(0.8 * n(N)) / np.sqrt(H) / u).astype(np.float32)
    w5_words, w5_scales = pack_weight(n((H, N)) / np.sqrt(H) / u, "e2m1")
    return {"tab_words": tab_words, "tab_scales": tab_scales, "offs": striped(np.random.permutation(T)[:S]),
            "w1": w1, "w2_words": w2_words, "w2_scales": w2_scales,
            "w3_words": w3_words, "w3_scales": w3_scales,
            "page0": page0, "wgs": wgs, "offs2": striped(np.random.permutation(T2)[:S]),
            "offs3": striped(np.random.permutation(T2)[:P]), "offs4": striped(np.random.permutation(T2)[:P]),
            "w4": w4, "w5_words": w5_words, "w5_scales": w5_scales}

def reference(tab_words, tab_scales, offs, w1, w2_words, w2_scales, w3_words, w3_scales,
              page0, wgs, offs2, offs3, offs4, w4, w5_words, w5_scales):
    v = unpack_weight(tab_words, tab_scales, "e4m3")[:, unstriped(offs)]
    a = mxq(f64(w1), 0, "e4m3").T @ v
    b = unpack_weight(w2_words, w2_scales, "e2m1").T @ v
    c = unpack_weight(w3_words, w3_scales, "e4m3").T @ v
    h = a * b * c
    page = f64(page0).copy()
    page[:, unstriped(offs2)] = np.tile(f64(wgs), (H // 128, 1)) * h
    z = page[:, unstriped(offs3)] + page[:, unstriped(offs4)]
    zq = mxq(z, 0, "e4m3")
    d = mxq(f64(w4), 0, "e4m3").T @ zq
    e = unpack_weight(w5_words, w5_scales, "e2m1").T @ zq
    y = d * e
    words, scales = planes(y)
    return y, words, scales

@@ -1,0 +1,362 @@
+from contextlib import ExitStack
+
+import concourse.mybir as mybir
+from concourse.masks import make_identity
+
+K, T, H, S, T2, M, N = 512, 2048, 1024, 1024, 2048, 1024, 512
+FLOPS = 2 * (3 * K * H * S + 2 * H * N * M)
+
+F32 = mybir.dt.float32
+BF16 = mybir.dt.bfloat16
+I32 = mybir.dt.int32
+U32 = mybir.dt.uint32
+U16 = mybir.dt.uint16
+U8 = mybir.dt.uint8
+FP8X4 = mybir.dt.float8_e4m3fn_x4
+FP4X4 = mybir.dt.float4_e2m1fn_x4
+MULT = mybir.AluOpType.mult
+
+P = 128
+BANK = 512
+ROW_TILES = H // P
+PASSES = H // 512
+W1_CHUNKS = ((0, 128), (128, 128), (256, 256), (512, 512))
+CHUNK = 256
+CHUNKS = M // CHUNK
+PICK_TILES = 3
+
+
+def tile_list_skat_trick_cubic_kernel(
+    tc, tab_words, tab_scales, offs, w1, w2_words, w2_scales, w3_words, w3_scales,
+    page0, wgs, offs2, offs3, offs4, w4, w5_words, w5_scales, out_0, out_1, out_2,
+):
+    nc = tc.nc
+    with ExitStack() as ctx:
+        lists = ctx.enter_context(tc.tile_pool(name="lists", bufs=1))
+        keep = ctx.enter_context(tc.tile_pool(name="keep", bufs=1))
+        psum = ctx.enter_context(tc.psum_pool(name="psum", bufs=1))
+
+        def sb(name, shape, dtype, tag=None):
+            return keep.tile(shape, dtype, name=name, tag=tag or name, align_bytes=64)
+
+        def load_list(name, src):
+            tile = lists.tile([P, 64], U16, name=name)
+            nc.sync.dma_start(tile[:], src)
+            return tile
+
+        def load_plane(plane, scales, queue):
+            passes = scales.shape[0]
+            for q in range(4):
+                queue.dma_start(
+                    plane[32 * q : 32 * q + 4, :].bitcast(I32).rearrange("r (a c) -> r a c", a=passes),
+                    scales[:, 4 * q : 4 * q + 4, :].bitcast(I32).rearrange("a r c -> r a c"),
+                )
+
+        mm_banks = [psum.tile([P, BANK], F32, name=f"mm_bank{b}") for b in range(4)]
+        sum_banks = [psum.tile([P, BANK], F32, name=f"sum_bank{b}") for b in range(2)]
+        back_banks = [psum.tile([P, BANK], F32, name=f"back_bank{b}") for b in range(2)]
+        turns = {"mm": 0, "sum": 0, "back": 0, "pick": 0, "late": 0}
+
+        def take(kind, tiles):
+            tile = tiles[turns[kind] % len(tiles)]
+            turns[kind] = turns[kind] + 1
+            return tile
+
+        tab_w = sb("tab_w", [P, T], U32)
+        tab_s = sb("tab_s", [P, T], U8)
+        w2_w = sb("w2_w", [P, 2 * H], U8)
+        w2_s = sb("w2_s", [P, H], U8)
+        w3_w = sb("w3_w", [P, H], U32)
+        w3_s = sb("w3_s", [P, H], U8)
+        w5_w = sb("w5_w", [P, PASSES * 2 * N], U8)
+        w5_s = sb("w5_s", [P, PASSES * N], U8)
+        for plane in (tab_s, w3_s, w5_s):
+            nc.vector.memset(plane[:].bitcast(I32), 0)
+        nc.gpsimd.memset(w2_s[:].bitcast(I32), 0)
+        load_plane(w2_s, w2_scales, nc.gpsimd)
+        ident = sb("ident", [P, P], F32)
+        make_identity(nc, ident[:])
+
+        w1_rows = w1.rearrange("(p j) c -> p j c", j=4)
+        w1_tags = ("w1_raw0", "w1_raw1", "stage_4k", "stage_8k")
+        w1_raw = [sb(f"w1_raw{n}", [P, 4, width], F32, w1_tags[n]) for n, (c0, width) in enumerate(W1_CHUNKS)]
+
+        def load_w1(n):
+            c0, width = W1_CHUNKS[n]
+            nc.sync.dma_start(w1_raw[n][:], w1_rows[:, :, c0 : c0 + width])
+
+        pages = [sb(f"page{i}", [P, T2], F32) for i in range(ROW_TILES)]
+
+        def load_page(i):
+            nc.sync.dma_start(pages[i][:], page0[P * i : P * (i + 1), :])
+
+        idx = load_list("idx", offs)
+        idx2 = load_list("idx2", offs2)
+        idx3 = load_list("idx3", offs3)
+        idx4 = load_list("idx4", offs4)
+        nc.sync.dma_start(tab_w[:].bitcast(I32), tab_words[0].rearrange("p t i -> p (t i)").bitcast(I32))
+        load_plane(tab_s, tab_scales, nc.scalar)
+        load_w1(0)
+        nc.sync.dma_start(w2_w[:].bitcast(I32), w2_words[0].bitcast(I32))
+        nc.sync.dma_start(w3_w[:].bitcast(I32), w3_words[0].rearrange("p c i -> p (c i)").bitcast(I32))
+        load_plane(w3_s, w3_scales, nc.sync)
+        wgs_sb = sb("wgs_sb", [P, S], F32)
+        nc.sync.dma_start(wgs_sb[:], wgs)
+        load_w1(1)
+        load_plane(w5_s, w5_scales, nc.sync)
+        nc.sync.dma_start(
+            w5_w[:].bitcast(I32).rearrange("p (a c) -> p a c", a=PASSES),
+            w5_words.bitcast(I32).rearrange("a p c -> p a c"),
+        )
+        load_page(0)
+        load_w1(2)
+        load_page(1)
+        load_w1(3)
+        load_page(2)
+        w4_rows = w4.rearrange("(a p j) n -> a p j n", a=PASSES, j=4)
+        w4_raw = [sb(f"w4_raw{a}", [P, 4, N], F32) for a in range(PASSES)]
+        for a in range(PASSES):
+            nc.sync.dma_start(w4_raw[a][:], w4_rows[a])
+        for i in range(3, ROW_TILES):
+            load_page(i)
+
+        v_w = sb("v_w", [P, S], U32)
+        v_s = sb("v_s", [P, S], U8)
+
+        def gather_table(half):
+            cols = slice(BANK * half, BANK * (half + 1))
+            entries = idx[:, 32 * half : 32 * (half + 1)]
+            nc.vector.tensor_copy(v_w[:, cols], tab_w[:].indirect(entries))
+            nc.vector.tensor_copy(v_s[:, cols], tab_s[:].indirect(entries))
+
+        w1_c = sb("w1_c", [P, H], U32)
+        w1_s = sb("w1_s", [P, H], U8)
+
+        def interleave(dst, src, mover):
+            mover(
+                dst.rearrange("p (c i t) -> p c t i", i=4, t=4),
+                src.rearrange("p t (c i) -> p c t i", i=4),
+            )
+
+        def quantise_w1(n):
+            c0, width = W1_CHUNKS[n]
+            grouped = sb(f"w1_bf{n}", [P, 4 * width], BF16, f"bf{n % 2}")
+            interleave(grouped[:], w1_raw[n][:], nc.scalar.copy)
+            nc.vector.quantize_mx(w1_c[:, c0 : c0 + width].bitcast(FP8X4), w1_s[:, c0 : c0 + width], grouped[:])
+
+        w4_c = sb("w4_c", [P, PASSES * N], U32)
+        w4_s = sb("w4_s", [P, PASSES * N], U8)
+
+        def quantise_w4(a):
+            grouped = sb(f"w4_bf{a}", [P, 4 * N], BF16, f"bf{a % 2}")
+            nc.scalar.copy(
+                grouped[:].rearrange("p (t m j) -> p m t j", t=4, j=4),
+                w4_raw[a][:].rearrange("p j (m t) -> p m t j", t=4),
+            )
+            cols = slice(N * a, N * (a + 1))
+            nc.vector.quantize_mx(w4_c[:, cols].bitcast(FP8X4), w4_s[:, cols], grouped[:])
+
+        w5_dw = sb("w5_dw", [P, PASSES * 2 * N], U8)
+        w5_ds = sb("w5_ds", [P, PASSES * N], U8)
+
+        def deal_w5():
+            nc.vector.tensor_copy(
+                w5_dw[:].bitcast(U16).rearrange("p (a t m) -> p a t m", a=PASSES, t=4),
+                w5_w[:].bitcast(U16).rearrange("p (a m t) -> p a t m", a=PASSES, t=4),
+            )
+            nc.vector.tensor_copy(
+                w5_ds[:].rearrange("p (a t m) -> p a t m", a=PASSES, t=4),
+                w5_s[:].rearrange("p (a m t) -> p a t m", a=PASSES, t=4),
+            )
+
+        abc = [[sb(f"{x}{n}", [P, S], F32) for x in "abc"] for n in range(2)]
+        values = [sb(f"values{n}", [P, S], F32) for n in range(2)]
+        last_bank = {}
+
+        def product(i, which, j):
+            rows = slice(P * i, P * (i + 1))
+            codes, scales = (
+                (w1_c[:, rows].bitcast(FP8X4), w1_s[:, rows]),
+                (w2_w[:, 2 * P * i : 2 * P * (i + 1)].bitcast(FP4X4), w2_s[:, rows]),
+                (w3_w[:, rows].bitcast(FP8X4), w3_s[:, rows]),
+            )[which]
+            cols = slice(j, j + BANK)
+            bank = take("mm", mm_banks)
+            nc.tensor.matmul_mx(
+                bank[:], lhsT=codes, lhsT_scale=scales,
+                rhs=v_w[:, cols].bitcast(FP8X4), rhs_scale=v_s[:, cols], start=True, stop=True,
+            )
+            last_bank[i] = bank
+            return bank
+
+        def first_values_on_vector():
+            a_sb, b_sb, c_sb = abc[0]
+            cols = slice(0, BANK)
+            nc.scalar.copy(b_sb[:, cols], product(0, 1, 0)[:])
+            nc.vector.tensor_tensor(c_sb[:, cols], product(0, 2, 0)[:], wgs_sb[:, cols], MULT)
+            nc.vector.tensor_tensor(a_sb[:, cols], product(0, 0, 0)[:], b_sb[:, cols], MULT)
+            nc.vector.tensor_tensor(values[0][:, cols], a_sb[:, cols], c_sb[:, cols], MULT)
+
+        def first_stage(i, j0):
+            a_sb, b_sb, c_sb = abc[i % 2]
+            for which in (1, 2, 0):
+                for j in range(j0, S, BANK):
+                    nc.scalar.copy(abc[i % 2][which][:, j : j + BANK], product(i, which, j)[:])
+            nc.gpsimd.tensor_tensor(b_sb[:, j0:], b_sb[:, j0:], c_sb[:, j0:], MULT)
+            nc.gpsimd.tensor_tensor(a_sb[:, j0:], a_sb[:, j0:], wgs_sb[:, j0:], MULT)
+
+        def finish_values(i, j0):
+            a_sb, b_sb, c_sb = abc[i % 2]
+            nc.gpsimd.tensor_tensor(values[i % 2][:, j0:], a_sb[:, j0:], b_sb[:, j0:], MULT)
+
+        def scatter(i, step):
+            for j0 in range(0, S, step):
+                entries = idx2[:, j0 // 16 : (j0 + step) // 16]
+                nc.vector.tensor_copy(pages[i][:].indirect(entries), values[i % 2][:, j0 : j0 + step])
+
+        picks = [sb(f"pick{n}", [P, BANK], F32)[:] for n in range(PICK_TILES)]
+        late_picks = [tile[:, j : j + BANK] for tile in (abc[1][0], abc[1][1], values[1]) for j in (0, BANK)]
+        z_t = [[sb(f"z_t{n}_{a}", [P, CHUNK // P, 2, P, 2], BF16) for a in range(PASSES)] for n in range(2)]
+
+        def sum_picks(i, n, both):
+            entries = slice(CHUNK * n // 16, CHUNK * (n + 1) // 16)
+            lead, answer = both[:, :CHUNK], both[:, CHUNK:]
+            nc.vector.tensor_copy(lead, pages[i][:].indirect(idx3[:, entries]))
+            nc.vector.tensor_copy(answer, pages[i][:].indirect(idx4[:, entries]))
+            bank = last_bank[i + 2] if n == 0 and i + 2 in last_bank else take("sum", sum_banks)
+            for m in range(0, CHUNK, P):
+                cols = slice(m, m + P)
+                nc.tensor.matmul(bank[:, cols], lead[:, cols], ident[:], start=True, stop=False, is_transpose=True)
+                nc.tensor.matmul(bank[:, cols], answer[:, cols], ident[:], start=False, stop=True, is_transpose=True)
+            q = i % 4
+            nc.scalar.copy(
+                z_t[n % 2][i // 4][:, :, :, 32 * q : 32 * (q + 1), :],
+                bank[:, :CHUNK].rearrange("m (b p u e) -> m b u p e", p=32, u=2, e=2),
+            )
+
+        z_i = [sb(f"z_i{n}", [P, 4 * CHUNK], F32) for n in range(2)]
+        z_c = sb("z_c", [P, PASSES * M], U32)
+        z_s = sb("z_s", [P, PASSES * M], U8)
+
+        def turn_back(n, a, b0, blocks):
+            bank = take("back", back_banks)
+            for b in range(blocks):
+                for u in range(2):
+                    col = P * (2 * b + u)
+                    src = z_t[n % 2][a][:, b0 + b, u].rearrange("m p e -> m (p e)").bitcast(F32)
+                    nc.tensor.transpose(bank[:, col : col + P], src, ident[:])
+            nc.scalar.copy(
+                z_i[n % 2][:].rearrange("p (b a m u) -> p b a m u", a=PASSES, m=P, u=2)[:, b0 : b0 + blocks, a],
+                bank[:, : 2 * P * blocks].rearrange("p (b u m) -> p b m u", u=2, m=P),
+            )
+
+        def quantise_z(n, b0, blocks):
+            cols = slice(PASSES * (CHUNK * n + P * b0), PASSES * (CHUNK * n + P * (b0 + blocks)))
+            words = z_i[n % 2][:, 4 * P * b0 : 4 * P * (b0 + blocks)]
+            nc.vector.quantize_mx(z_c[:, cols].bitcast(FP8X4), z_s[:, cols], words.bitcast(BF16))
+
+        y_c = sb("y_c", [P, M], U32)
+        y_s = sb("y_s", [P, M], U8)
+        y_rows = out_0.rearrange("(p t) m -> p t m", t=4)
+        y_words = out_1[0].rearrange("p m t -> p (m t)").bitcast(I32)
+
+        def second_products(m0):
+            banks = []
+            for codes, size, dtype, scales in ((w4_c, 1, FP8X4, w4_s), (w5_dw, 2, FP4X4, w5_ds)):
+                bank = take("mm", mm_banks)
+                for t in range(4):
+                    for a in range(PASSES):
+                        w0 = N * a + P * t
+                        cols = slice(PASSES * m0 + P * a, PASSES * m0 + P * (a + 1))
+                        nc.tensor.matmul_mx(
+                            bank[:, P * t : P * (t + 1)],
+                            lhsT=codes[:, size * w0 : size * (w0 + P)].bitcast(dtype), lhsT_scale=scales[:, w0 : w0 + P],
+                            rhs=z_c[:, cols].bitcast(FP8X4), rhs_scale=z_s[:, cols],
+                            start=(a == 0), stop=(a == PASSES - 1),
+                        )
+                banks.append(bank)
+            return banks
+
+        de_tiles = ((abc[0][0], abc[0][1]), (abc[0][2], abc[1][2]))
+
+        def y_tile(n):
+            return sb(f"y{n}", [P, 4, CHUNK], F32, ("stage_4k", "stage_8k")[n % 2])
+
+        def second_stage(n):
+            y = y_tile(n)
+            d_sb, e_sb = de_tiles[n % 2]
+            for b in range(CHUNK // P):
+                d_bank, e_bank = second_products(CHUNK * n + P * b)
+                nc.scalar.copy(d_sb[:, BANK * b : BANK * (b + 1)], d_bank[:])
+                nc.scalar.copy(e_sb[:, BANK * b : BANK * (b + 1)], e_bank[:])
+            nc.gpsimd.tensor_tensor(
+                y[:].rearrange("p t (b m) -> p b t m", m=P),
+                d_sb[:].rearrange("p (b t m) -> p b t m", t=4, m=P),
+                e_sb[:].rearrange("p (b t m) -> p b t m", t=4, m=P), MULT,
+            )
+            cols = slice(CHUNK * n, CHUNK * (n + 1))
+            nc.sync.dma_start(y_rows[:, :, cols], y[:])
+            grouped = sb(f"y_bf{n}", [P, 4 * CHUNK], BF16, f"bf{n % 2}")
+            interleave(grouped[:], y[:], nc.scalar.copy)
+            nc.vector.quantize_mx(y_c[:, cols].bitcast(FP8X4), y_s[:, cols], grouped[:])
+            nc.sync.dma_start(y_words[:, cols], y_c[:, cols].bitcast(I32))
+
+        def last_stage(n):
+            y = y_tile(n)
+            d_sb = de_tiles[n % 2][0]
+            grouped = sb(f"y_bf{n}", [P, 4 * CHUNK], BF16, f"bf{n % 2}")
+            for b in range(CHUNK // P):
+                turn_back(n, 1, b, 1)
+                quantise_z(n, b, 1)
+            for b in range(CHUNK // P):
+                d_bank, e_bank = second_products(CHUNK * n + P * b)
+                d_part = d_sb[:, BANK * b : BANK * (b + 1)]
+                y_part = y[:, :, P * b : P * (b + 1)]
+                nc.scalar.copy(d_part, d_bank[:])
+                nc.vector.tensor_tensor(
+                    y_part, e_bank[:].rearrange("p (t m) -> p t m", m=P), d_part.rearrange("p (t m) -> p t m", m=P), MULT
+                )
+                cols = slice(CHUNK * n + P * b, CHUNK * n + P * (b + 1))
+                nc.sync.dma_start(y_rows[:, :, cols], y_part)
+                interleave(grouped[:, BANK * b : BANK * (b + 1)], y_part, nc.vector.tensor_copy)
+                nc.vector.quantize_mx(y_c[:, cols].bitcast(FP8X4), y_s[:, cols], grouped[:, BANK * b : BANK * (b + 1)])
+            cols = slice(CHUNK * n, CHUNK * (n + 1))
+            nc.sync.dma_start(y_words[:, cols], y_c[:, cols].bitcast(I32))
+
+        gather_table(0)
+        quantise_w1(0)
+        gather_table(1)
+        first_values_on_vector()
+        first_stage(0, BANK)
+        finish_values(0, BANK)
+        quantise_w1(1)
+        deal_w5()
+        first_stage(1, 0)
+        finish_values(1, 0)
+        quantise_w1(2)
+        for i in range(ROW_TILES):
+            if i + 2 < ROW_TILES:
+                first_stage(i + 2, 0)
+            if i == 0:
+                quantise_w1(3)
+            scatter(i, BANK if i == 0 else S)
+            if i + 2 < ROW_TILES:
+                finish_values(i + 2, 0)
+            sum_picks(i, 0, take("pick", picks))
+            if i in (2, 3):
+                quantise_w4(i - 2)
+            if i % 4 == 3:
+                turn_back(0, i // 4, 0, 2)
+        for n in range(1, CHUNKS):
+            quantise_z(n - 1, 0, 2)
+            for i in range(ROW_TILES):
+                if i == 4:
+                    second_stage(n - 1)
+                    sum_picks(i, n, z_i[(n - 1) % 2][:, :BANK])
+                else:
+                    sum_picks(i, n, take("late", late_picks))
+                if i == 3 or (i == 7 and n + 1 < CHUNKS):
+                    turn_back(n, i // 4, 0, 2)
+        last_stage(CHUNKS - 1)
+        for q in range(4):
+            (nc.sync, nc.scalar)[q % 2].dma_start(out_2[0, 4 * q : 4 * q + 4, :].bitcast(I32), y_s[32 * q : 32 * q + 4, :].bitcast(I32))

@@ -23,7 +23,7 @@ PASSES = H // 512
 W1_CHUNKS = ((0, 128), (128, 128), (256, 256), (512, 512))
 CHUNK = 256
 CHUNKS = M // CHUNK
-PICK_TILES = 3
+PICK_TILES = 4
 
 
 def tile_list_skat_trick_cubic_kernel(
@@ -108,8 +108,8 @@ def tile_list_skat_trick_cubic_kernel(
             w5_w[:].bitcast(I32).rearrange("p (a c) -> p a c", a=PASSES),
             w5_words.bitcast(I32).rearrange("a p c -> p a c"),
         )
-        load_page(0)
         load_w1(2)
+        load_page(0)
         load_page(1)
         load_w1(3)
         load_page(2)
@@ -129,7 +129,7 @@ def tile_list_skat_trick_cubic_kernel(
             nc.vector.tensor_copy(v_w[:, cols], tab_w[:].indirect(entries))
             nc.vector.tensor_copy(v_s[:, cols], tab_s[:].indirect(entries))
 
-        w1_c = sb("w1_c", [P, H], U32)
+        w1_c = {}
         w1_s = sb("w1_s", [P, H], U8)
 
         def interleave(dst, src, mover):
@@ -142,19 +142,23 @@ def tile_list_skat_trick_cubic_kernel(
             c0, width = W1_CHUNKS[n]
             grouped = sb(f"w1_bf{n}", [P, 4 * width], BF16, f"bf{n % 2}")
             interleave(grouped[:], w1_raw[n][:], nc.scalar.copy)
-            nc.vector.quantize_mx(w1_c[:, c0 : c0 + width].bitcast(FP8X4), w1_s[:, c0 : c0 + width], grouped[:])
+            codes = sb(f"w1_c{n}", [P, width], U32)
+            nc.vector.quantize_mx(codes[:].bitcast(FP8X4), w1_s[:, c0 : c0 + width], grouped[:])
+            for c in range(0, width, P):
+                w1_c[(c0 + c) // P] = codes[:, c : c + P]
 
-        w4_c = sb("w4_c", [P, PASSES * N], U32)
+        w4_c = {}
         w4_s = sb("w4_s", [P, PASSES * N], U8)
 
         def quantise_w4(a):
-            grouped = sb(f"w4_bf{a}", [P, 4 * N], BF16, f"bf{a % 2}")
+            grouped = sb(f"w4_bf{a}", [P, 4 * N], BF16, "bf0")
             nc.scalar.copy(
                 grouped[:].rearrange("p (t m j) -> p m t j", t=4, j=4),
                 w4_raw[a][:].rearrange("p j (m t) -> p m t j", t=4),
             )
             cols = slice(N * a, N * (a + 1))
-            nc.vector.quantize_mx(w4_c[:, cols].bitcast(FP8X4), w4_s[:, cols], grouped[:])
+            w4_c[a] = sb(f"w4_c{a}", [P, N], U32)
+            nc.vector.quantize_mx(w4_c[a][:].bitcast(FP8X4), w4_s[:, cols], grouped[:])
 
         w5_dw = sb("w5_dw", [P, PASSES * 2 * N], U8)
         w5_ds = sb("w5_ds", [P, PASSES * N], U8)
@@ -170,13 +174,20 @@ def tile_list_skat_trick_cubic_kernel(
             )
 
         abc = [[sb(f"{x}{n}", [P, S], F32) for x in "abc"] for n in range(2)]
-        values = [sb(f"values{n}", [P, S], F32) for n in range(2)]
+        value_tags = ("v0", "w1_c3", "v1", "w4_c0", "w4_c1", "v0", "v1", "v0")
+        values = {}
+
+        def value_tile(i):
+            if i not in values:
+                values[i] = sb(f"values{i}", [P, S], F32, value_tags[i])
+            return values[i]
+
         last_bank = {}
 
         def product(i, which, j):
             rows = slice(P * i, P * (i + 1))
             codes, scales = (
-                (w1_c[:, rows].bitcast(FP8X4), w1_s[:, rows]),
+                (w1_c[i].bitcast(FP8X4), w1_s[:, rows]),
                 (w2_w[:, 2 * P * i : 2 * P * (i + 1)].bitcast(FP4X4), w2_s[:, rows]),
                 (w3_w[:, rows].bitcast(FP8X4), w3_s[:, rows]),
             )[which]
@@ -192,10 +203,10 @@ def tile_list_skat_trick_cubic_kernel(
         def first_values_on_vector():
             a_sb, b_sb, c_sb = abc[0]
             cols = slice(0, BANK)
-            nc.scalar.copy(b_sb[:, cols], product(0, 1, 0)[:])
+            nc.scalar.copy(a_sb[:, cols], product(0, 0, 0)[:])
             nc.vector.tensor_tensor(c_sb[:, cols], product(0, 2, 0)[:], wgs_sb[:, cols], MULT)
-            nc.vector.tensor_tensor(a_sb[:, cols], product(0, 0, 0)[:], b_sb[:, cols], MULT)
-            nc.vector.tensor_tensor(values[0][:, cols], a_sb[:, cols], c_sb[:, cols], MULT)
+            nc.vector.tensor_tensor(b_sb[:, cols], product(0, 1, 0)[:], a_sb[:, cols], MULT)
+            nc.vector.tensor_tensor(value_tile(0)[:, cols], b_sb[:, cols], c_sb[:, cols], MULT)
 
         def first_stage(i, j0):
             a_sb, b_sb, c_sb = abc[i % 2]
@@ -207,48 +218,58 @@ def tile_list_skat_trick_cubic_kernel(
 
         def finish_values(i, j0):
             a_sb, b_sb, c_sb = abc[i % 2]
-            nc.gpsimd.tensor_tensor(values[i % 2][:, j0:], a_sb[:, j0:], b_sb[:, j0:], MULT)
+            nc.gpsimd.tensor_tensor(value_tile(i)[:, j0:], a_sb[:, j0:], b_sb[:, j0:], MULT)
 
         def scatter(i, step):
             for j0 in range(0, S, step):
                 entries = idx2[:, j0 // 16 : (j0 + step) // 16]
-                nc.vector.tensor_copy(pages[i][:].indirect(entries), values[i % 2][:, j0 : j0 + step])
+                nc.vector.tensor_copy(pages[i][:].indirect(entries), values[i][:, j0 : j0 + step])
 
-        picks = [sb(f"pick{n}", [P, BANK], F32)[:] for n in range(PICK_TILES)]
-        late_picks = [tile[:, j : j + BANK] for tile in (abc[1][0], abc[1][1], values[1]) for j in (0, BANK)]
-        z_t = [[sb(f"z_t{n}_{a}", [P, CHUNK // P, 2, P, 2], BF16) for a in range(PASSES)] for n in range(2)]
+        picks = [sb(f"pick{n}", [P, BANK], F32) for n in range(PICK_TILES)]
+        z_t = [[sb(f"z_t{a}_{half}", [P, 4, 2, P, 2], BF16) for half in range(2)] for a in range(PASSES)]
 
-        def sum_picks(i, n, both):
-            entries = slice(CHUNK * n // 16, CHUNK * (n + 1) // 16)
-            lead, answer = both[:, :CHUNK], both[:, CHUNK:]
+        def sum_picks(i, m0, width, lead, answer, bank):
+            entries = slice(m0 // 16, (m0 + width) // 16)
             nc.vector.tensor_copy(lead, pages[i][:].indirect(idx3[:, entries]))
             nc.vector.tensor_copy(answer, pages[i][:].indirect(idx4[:, entries]))
-            bank = last_bank[i + 2] if n == 0 and i + 2 in last_bank else take("sum", sum_banks)
-            for m in range(0, CHUNK, P):
+            for m in range(0, width, P):
                 cols = slice(m, m + P)
-                nc.tensor.matmul(bank[:, cols], lead[:, cols], ident[:], start=True, stop=False, is_transpose=True)
-                nc.tensor.matmul(bank[:, cols], answer[:, cols], ident[:], start=False, stop=True, is_transpose=True)
+                nc.tensor.matmul(bank[:, cols], lead[:, cols], ident[:], start=(m == 0), stop=False, is_transpose=True)
+            for m in range(0, width, P):
+                cols = slice(m, m + P)
+                nc.tensor.matmul(
+                    bank[:, cols], answer[:, cols], ident[:], start=False, stop=(m + P == width), is_transpose=True
+                )
             q = i % 4
+            b0 = m0 // P % 4
             nc.scalar.copy(
-                z_t[n % 2][i // 4][:, :, :, 32 * q : 32 * (q + 1), :],
-                bank[:, :CHUNK].rearrange("m (b p u e) -> m b u p e", p=32, u=2, e=2),
+                z_t[i // 4][m0 // BANK][:, b0 : b0 + width // P, :, 32 * q : 32 * (q + 1), :],
+                bank[:, :width].rearrange("m (b p u e) -> m b u p e", p=32, u=2, e=2),
             )
 
+        def late_pick(n, i, slot):
+            sum_picks(i, CHUNK * n, CHUNK, slot[:, :CHUNK], slot[:, CHUNK:], take("sum", sum_banks))
+
+        def late_picks(n, i0, slots):
+            for k in range(2):
+                late_pick(n, i0 + k, slots[:, BANK * k : BANK * (k + 1)])
+
         z_i = [sb(f"z_i{n}", [P, 4 * CHUNK], F32) for n in range(2)]
-        z_c = sb("z_c", [P, PASSES * M], U32)
-        z_s = sb("z_s", [P, PASSES * M], U8)
 
         def turn_back(n, a, b0, blocks):
             bank = take("back", back_banks)
             for b in range(blocks):
                 for u in range(2):
                     col = P * (2 * b + u)
-                    src = z_t[n % 2][a][:, b0 + b, u].rearrange("m p e -> m (p e)").bitcast(F32)
+                    src = z_t[a][n // 2][:, 2 * (n % 2) + b0 + b, u].rearrange("m p e -> m (p e)").bitcast(F32)
                     nc.tensor.transpose(bank[:, col : col + P], src, ident[:])
             nc.scalar.copy(
                 z_i[n % 2][:].rearrange("p (b a m u) -> p b a m u", a=PASSES, m=P, u=2)[:, b0 : b0 + blocks, a],
                 bank[:, : 2 * P * blocks].rearrange("p (b u m) -> p b m u", u=2, m=P),
             )
+
+        z_c = sb("z_c", [P, PASSES * M], U32)
+        z_s = sb("z_s", [P, PASSES * M], U8)
 
         def quantise_z(n, b0, blocks):
             cols = slice(PASSES * (CHUNK * n + P * b0), PASSES * (CHUNK * n + P * (b0 + blocks)))
@@ -262,66 +283,51 @@ def tile_list_skat_trick_cubic_kernel(
 
         def second_products(m0):
             banks = []
-            for codes, size, dtype, scales in ((w4_c, 1, FP8X4, w4_s), (w5_dw, 2, FP4X4, w5_ds)):
+            for scales in (w4_s, w5_ds):
                 bank = take("mm", mm_banks)
                 for t in range(4):
                     for a in range(PASSES):
                         w0 = N * a + P * t
                         cols = slice(PASSES * m0 + P * a, PASSES * m0 + P * (a + 1))
+                        if not banks:
+                            codes = w4_c[a][:, P * t : P * (t + 1)].bitcast(FP8X4)
+                        else:
+                            codes = w5_dw[:, 2 * w0 : 2 * (w0 + P)].bitcast(FP4X4)
                         nc.tensor.matmul_mx(
                             bank[:, P * t : P * (t + 1)],
-                            lhsT=codes[:, size * w0 : size * (w0 + P)].bitcast(dtype), lhsT_scale=scales[:, w0 : w0 + P],
+                            lhsT=codes, lhsT_scale=scales[:, w0 : w0 + P],
                             rhs=z_c[:, cols].bitcast(FP8X4), rhs_scale=z_s[:, cols],
                             start=(a == 0), stop=(a == PASSES - 1),
                         )
                 banks.append(bank)
             return banks
 
-        de_tiles = ((abc[0][0], abc[0][1]), (abc[0][2], abc[1][2]))
+        y = {}
 
-        def y_tile(n):
-            return sb(f"y{n}", [P, 4, CHUNK], F32, ("stage_4k", "stage_8k")[n % 2])
-
-        def second_stage(n):
-            y = y_tile(n)
-            d_sb, e_sb = de_tiles[n % 2]
-            for b in range(CHUNK // P):
-                d_bank, e_bank = second_products(CHUNK * n + P * b)
-                nc.scalar.copy(d_sb[:, BANK * b : BANK * (b + 1)], d_bank[:])
-                nc.scalar.copy(e_sb[:, BANK * b : BANK * (b + 1)], e_bank[:])
-            nc.gpsimd.tensor_tensor(
-                y[:].rearrange("p t (b m) -> p b t m", m=P),
-                d_sb[:].rearrange("p (b t m) -> p b t m", t=4, m=P),
-                e_sb[:].rearrange("p (b t m) -> p b t m", t=4, m=P), MULT,
+        def y_block(n, b, tag):
+            if b == 0:
+                y[n] = sb(f"y{n}", [P, 4, CHUNK], F32, ("stage_4k", "stage_8k")[n % 2])
+            d_bank, e_bank = second_products(CHUNK * n + P * b)
+            d_sb = sb(f"d{n}_{b}", [P, 4, P], F32, tag)
+            nc.scalar.copy(d_sb[:].rearrange("p t m -> p (t m)"), d_bank[:])
+            nc.vector.tensor_tensor(
+                y[n][:, :, P * b : P * (b + 1)], e_bank[:].rearrange("p (t m) -> p t m", m=P), d_sb[:], MULT
             )
-            cols = slice(CHUNK * n, CHUNK * (n + 1))
-            nc.sync.dma_start(y_rows[:, :, cols], y[:])
-            grouped = sb(f"y_bf{n}", [P, 4 * CHUNK], BF16, f"bf{n % 2}")
-            interleave(grouped[:], y[:], nc.scalar.copy)
+
+        def hand_out(n, b0, blocks, mover):
+            part = y[n][:, :, P * b0 : P * (b0 + blocks)]
+            cols = slice(CHUNK * n + P * b0, CHUNK * n + P * (b0 + blocks))
+            nc.sync.dma_start(y_rows[:, :, cols], part)
+            grouped = sb(f"y_bf{n}_{b0}", [P, 4 * P * blocks], BF16, f"bf{(n + b0) % 2}")
+            interleave(grouped[:], part, mover)
             nc.vector.quantize_mx(y_c[:, cols].bitcast(FP8X4), y_s[:, cols], grouped[:])
+
+        def store_words(n):
+            cols = slice(CHUNK * n, CHUNK * (n + 1))
             nc.sync.dma_start(y_words[:, cols], y_c[:, cols].bitcast(I32))
 
-        def last_stage(n):
-            y = y_tile(n)
-            d_sb = de_tiles[n % 2][0]
-            grouped = sb(f"y_bf{n}", [P, 4 * CHUNK], BF16, f"bf{n % 2}")
-            for b in range(CHUNK // P):
-                turn_back(n, 1, b, 1)
-                quantise_z(n, b, 1)
-            for b in range(CHUNK // P):
-                d_bank, e_bank = second_products(CHUNK * n + P * b)
-                d_part = d_sb[:, BANK * b : BANK * (b + 1)]
-                y_part = y[:, :, P * b : P * (b + 1)]
-                nc.scalar.copy(d_part, d_bank[:])
-                nc.vector.tensor_tensor(
-                    y_part, e_bank[:].rearrange("p (t m) -> p t m", m=P), d_part.rearrange("p (t m) -> p t m", m=P), MULT
-                )
-                cols = slice(CHUNK * n + P * b, CHUNK * n + P * (b + 1))
-                nc.sync.dma_start(y_rows[:, :, cols], y_part)
-                interleave(grouped[:, BANK * b : BANK * (b + 1)], y_part, nc.vector.tensor_copy)
-                nc.vector.quantize_mx(y_c[:, cols].bitcast(FP8X4), y_s[:, cols], grouped[:, BANK * b : BANK * (b + 1)])
-            cols = slice(CHUNK * n, CHUNK * (n + 1))
-            nc.sync.dma_start(y_words[:, cols], y_c[:, cols].bitcast(I32))
+        def slots(name, tag):
+            return sb(name, [P, S], F32, tag)
 
         gather_table(0)
         quantise_w1(0)
@@ -337,26 +343,51 @@ def tile_list_skat_trick_cubic_kernel(
         for i in range(ROW_TILES):
             if i + 2 < ROW_TILES:
                 first_stage(i + 2, 0)
-            if i == 0:
-                quantise_w1(3)
             scatter(i, BANK if i == 0 else S)
+            if i == 1:
+                quantise_w1(3)
+            if i in (3, 4):
+                quantise_w4(i - 3)
             if i + 2 < ROW_TILES:
                 finish_values(i + 2, 0)
-            sum_picks(i, 0, take("pick", picks))
-            if i in (2, 3):
-                quantise_w4(i - 2)
+            bank = last_bank[i + 2] if i + 2 < ROW_TILES else take("sum", sum_banks)
+            lead, answer = take("pick", picks)[:], take("pick", picks)[:]
+            sum_picks(i, 0, BANK, lead, answer, bank)
+            if i < 2:
+                sum_picks(i, BANK, BANK, take("pick", picks)[:], take("pick", picks)[:], take("sum", sum_banks))
             if i % 4 == 3:
                 turn_back(0, i // 4, 0, 2)
-        for n in range(1, CHUNKS):
-            quantise_z(n - 1, 0, 2)
-            for i in range(ROW_TILES):
-                if i == 4:
-                    second_stage(n - 1)
-                    sum_picks(i, n, z_i[(n - 1) % 2][:, :BANK])
-                else:
-                    sum_picks(i, n, take("late", late_picks))
-                if i == 3 or (i == 7 and n + 1 < CHUNKS):
-                    turn_back(n, i // 4, 0, 2)
-        last_stage(CHUNKS - 1)
+                turn_back(1, i // 4, 0, 2)
+        for i in range(2, 6):
+            late_pick(2, i, (lead, answer)[i % 2])
+        quantise_z(0, 0, 2)
+        quantise_z(1, 0, 2)
+        turn_back(2, 0, 0, 2)
+        y_block(0, 0, "a0")
+        y_block(0, 1, "b0")
+        late_picks(2, 6, z_i[1])
+        turn_back(2, 1, 0, 2)
+        late_picks(3, 2, slots("late_b", "a0"))
+        quantise_z(2, 0, 2)
+        hand_out(0, 0, 2, nc.scalar.copy)
+        store_words(0)
+        y_block(1, 0, "c0")
+        y_block(1, 1, "c1")
+        turn_back(3, 0, 0, 2)
+        late_picks(3, 4, slots("late_d", "c0"))
+        hand_out(1, 0, 2, nc.scalar.copy)
+        store_words(1)
+        y_block(2, 0, "b1")
+        late_picks(3, 6, slots("late_e", "c1"))
+        y_block(2, 1, "a1")
+        for b in range(2):
+            turn_back(3, 1, b, 1)
+            quantise_z(3, b, 1)
+        hand_out(2, 0, 2, nc.scalar.copy)
+        store_words(2)
+        for b in range(2):
+            y_block(3, b, ("a0", "b0")[b])
+            hand_out(3, b, 1, nc.vector.tensor_copy)
+        store_words(3)
         for q in range(4):
             (nc.sync, nc.scalar)[q % 2].dma_start(out_2[0, 4 * q : 4 * q + 4, :].bitcast(I32), y_s[32 * q : 32 * q + 4, :].bitcast(I32))

@@ -23,7 +23,6 @@ PASSES = H // 512
 W1_CHUNKS = ((0, 128), (128, 128), (256, 256), (512, 512))
 CHUNK = 256
 CHUNKS = M // CHUNK
-PICK_TILES = 4
 
 
 def tile_list_skat_trick_cubic_kernel(
@@ -91,25 +90,29 @@ def tile_list_skat_trick_cubic_kernel(
             nc.sync.dma_start(pages[i][:], page0[P * i : P * (i + 1), :])
 
         idx = load_list("idx", offs)
+        nc.sync.dma_start(tab_w[:].bitcast(I32), tab_words[0].rearrange("p t i -> p (t i)").bitcast(I32))
+        load_plane(tab_s, tab_scales, nc.sync)
+        load_w1(0)
+        w2_src = w2_words[0].bitcast(I32)
+        w3_src = w3_words[0].rearrange("p c i -> p (c i)").bitcast(I32)
+        nc.sync.dma_start(w2_w[:, : 2 * P].bitcast(I32), w2_src[:, : P // 2])
+        nc.sync.dma_start(w3_w[:, :P].bitcast(I32), w3_src[:, :P])
         idx2 = load_list("idx2", offs2)
         idx3 = load_list("idx3", offs3)
         idx4 = load_list("idx4", offs4)
-        nc.sync.dma_start(tab_w[:].bitcast(I32), tab_words[0].rearrange("p t i -> p (t i)").bitcast(I32))
-        load_plane(tab_s, tab_scales, nc.scalar)
-        load_w1(0)
-        nc.sync.dma_start(w2_w[:].bitcast(I32), w2_words[0].bitcast(I32))
-        nc.sync.dma_start(w3_w[:].bitcast(I32), w3_words[0].rearrange("p c i -> p (c i)").bitcast(I32))
         load_plane(w3_s, w3_scales, nc.sync)
         wgs_sb = sb("wgs_sb", [P, S], F32)
         nc.sync.dma_start(wgs_sb[:], wgs)
         load_w1(1)
+        nc.sync.dma_start(w2_w[:, 2 * P :].bitcast(I32), w2_src[:, P // 2 :])
+        nc.sync.dma_start(w3_w[:, P:].bitcast(I32), w3_src[:, P:])
+        load_page(0)
+        load_w1(2)
         load_plane(w5_s, w5_scales, nc.sync)
         nc.sync.dma_start(
             w5_w[:].bitcast(I32).rearrange("p (a c) -> p a c", a=PASSES),
             w5_words.bitcast(I32).rearrange("a p c -> p a c"),
         )
-        load_w1(2)
-        load_page(0)
         load_page(1)
         load_w1(3)
         load_page(2)
@@ -173,16 +176,20 @@ def tile_list_skat_trick_cubic_kernel(
                 w5_s[:].rearrange("p (a m t) -> p a t m", a=PASSES, t=4),
             )
 
-        abc = [[sb(f"{x}{n}", [P, S], F32) for x in "abc"] for n in range(2)]
+        a_tiles = [sb(f"a{n}", [P, S], F32) for n in range(2)]
+        b_tiles = [sb(f"b{n}", [P, S], F32) for n in range(3)]
+        c_tiles = [sb(f"c{n}", [P, S], F32) for n in range(2)]
         value_tags = ("v0", "w1_c3", "v1", "w4_c0", "w4_c1", "v0", "v1", "v0")
         values = {}
+        last_bank = {}
+
+        def abc(i):
+            return a_tiles[i % 2], b_tiles[i % 3], c_tiles[i % 2]
 
         def value_tile(i):
             if i not in values:
                 values[i] = sb(f"values{i}", [P, S], F32, value_tags[i])
             return values[i]
-
-        last_bank = {}
 
         def product(i, which, j):
             rows = slice(P * i, P * (i + 1))
@@ -201,7 +208,7 @@ def tile_list_skat_trick_cubic_kernel(
             return bank
 
         def first_values_on_vector():
-            a_sb, b_sb, c_sb = abc[0]
+            a_sb, b_sb, c_sb = abc(0)
             cols = slice(0, BANK)
             nc.scalar.copy(a_sb[:, cols], product(0, 0, 0)[:])
             nc.vector.tensor_tensor(c_sb[:, cols], product(0, 2, 0)[:], wgs_sb[:, cols], MULT)
@@ -209,15 +216,15 @@ def tile_list_skat_trick_cubic_kernel(
             nc.vector.tensor_tensor(value_tile(0)[:, cols], b_sb[:, cols], c_sb[:, cols], MULT)
 
         def first_stage(i, j0):
-            a_sb, b_sb, c_sb = abc[i % 2]
+            a_sb, b_sb, c_sb = abc(i)
             for which in (1, 2, 0):
                 for j in range(j0, S, BANK):
-                    nc.scalar.copy(abc[i % 2][which][:, j : j + BANK], product(i, which, j)[:])
+                    nc.scalar.copy(abc(i)[which][:, j : j + BANK], product(i, which, j)[:])
             nc.gpsimd.tensor_tensor(b_sb[:, j0:], b_sb[:, j0:], c_sb[:, j0:], MULT)
             nc.gpsimd.tensor_tensor(a_sb[:, j0:], a_sb[:, j0:], wgs_sb[:, j0:], MULT)
 
         def finish_values(i, j0):
-            a_sb, b_sb, c_sb = abc[i % 2]
+            a_sb, b_sb, c_sb = abc(i)
             nc.gpsimd.tensor_tensor(value_tile(i)[:, j0:], a_sb[:, j0:], b_sb[:, j0:], MULT)
 
         def scatter(i, step):
@@ -225,10 +232,11 @@ def tile_list_skat_trick_cubic_kernel(
                 entries = idx2[:, j0 // 16 : (j0 + step) // 16]
                 nc.vector.tensor_copy(pages[i][:].indirect(entries), values[i][:, j0 : j0 + step])
 
-        picks = [sb(f"pick{n}", [P, BANK], F32) for n in range(PICK_TILES)]
         z_t = [[sb(f"z_t{a}_{half}", [P, 4, 2, P, 2], BF16) for half in range(2)] for a in range(PASSES)]
 
-        def sum_picks(i, m0, width, lead, answer, bank):
+        def sum_picks(i, m0, slot, bank):
+            width = slot.shape[1] // 2
+            lead, answer = slot[:, :width], slot[:, width:]
             entries = slice(m0 // 16, (m0 + width) // 16)
             nc.vector.tensor_copy(lead, pages[i][:].indirect(idx3[:, entries]))
             nc.vector.tensor_copy(answer, pages[i][:].indirect(idx4[:, entries]))
@@ -248,32 +256,26 @@ def tile_list_skat_trick_cubic_kernel(
             )
 
         def late_pick(n, i, slot):
-            sum_picks(i, CHUNK * n, CHUNK, slot[:, :CHUNK], slot[:, CHUNK:], take("sum", sum_banks))
+            sum_picks(i, CHUNK * n, slot, take("sum", sum_banks))
 
-        def late_picks(n, i0, slots):
-            for k in range(2):
-                late_pick(n, i0 + k, slots[:, BANK * k : BANK * (k + 1)])
-
-        z_i = [sb(f"z_i{n}", [P, 4 * CHUNK], F32) for n in range(2)]
-
-        def turn_back(n, a, b0, blocks):
+        def turn_back(a, m0, blocks, words, mover):
             bank = take("back", back_banks)
             for b in range(blocks):
                 for u in range(2):
                     col = P * (2 * b + u)
-                    src = z_t[a][n // 2][:, 2 * (n % 2) + b0 + b, u].rearrange("m p e -> m (p e)").bitcast(F32)
+                    src = z_t[a][m0 // BANK][:, m0 // P % 4 + b, u].rearrange("m p e -> m (p e)").bitcast(F32)
                     nc.tensor.transpose(bank[:, col : col + P], src, ident[:])
-            nc.scalar.copy(
-                z_i[n % 2][:].rearrange("p (b a m u) -> p b a m u", a=PASSES, m=P, u=2)[:, b0 : b0 + blocks, a],
-                bank[:, : 2 * P * blocks].rearrange("p (b u m) -> p b m u", u=2, m=P),
-            )
+            mover(words, bank[:, : 2 * P * blocks].rearrange("p (b u m) -> p b m u", u=2, m=P))
 
+        def by_block(words):
+            return words.rearrange("p (b m u) -> p b m u", m=P, u=2)
+
+        z_words = sb("z_words", [P, 2 * S], F32)
         z_c = sb("z_c", [P, PASSES * M], U32)
         z_s = sb("z_s", [P, PASSES * M], U8)
 
-        def quantise_z(n, b0, blocks):
-            cols = slice(PASSES * (CHUNK * n + P * b0), PASSES * (CHUNK * n + P * (b0 + blocks)))
-            words = z_i[n % 2][:, 4 * P * b0 : 4 * P * (b0 + blocks)]
+        def quantise_z(c0, words):
+            cols = slice(c0, c0 + words.shape[1] // 2)
             nc.vector.quantize_mx(z_c[:, cols].bitcast(FP8X4), z_s[:, cols], words.bitcast(BF16))
 
         y_c = sb("y_c", [P, M], U32)
@@ -281,53 +283,50 @@ def tile_list_skat_trick_cubic_kernel(
         y_rows = out_0.rearrange("(p t) m -> p t m", t=4)
         y_words = out_1[0].rearrange("p m t -> p (m t)").bitcast(I32)
 
-        def second_products(m0):
-            banks = []
-            for scales in (w4_s, w5_ds):
-                bank = take("mm", mm_banks)
-                for t in range(4):
-                    for a in range(PASSES):
-                        w0 = N * a + P * t
-                        cols = slice(PASSES * m0 + P * a, PASSES * m0 + P * (a + 1))
-                        if not banks:
-                            codes = w4_c[a][:, P * t : P * (t + 1)].bitcast(FP8X4)
-                        else:
-                            codes = w5_dw[:, 2 * w0 : 2 * (w0 + P)].bitcast(FP4X4)
-                        nc.tensor.matmul_mx(
-                            bank[:, P * t : P * (t + 1)],
-                            lhsT=codes, lhsT_scale=scales[:, w0 : w0 + P],
-                            rhs=z_c[:, cols].bitcast(FP8X4), rhs_scale=z_s[:, cols],
-                            start=(a == 0), stop=(a == PASSES - 1),
-                        )
-                banks.append(bank)
-            return banks
-
-        y = {}
-
-        def y_block(n, b, tag):
-            if b == 0:
-                y[n] = sb(f"y{n}", [P, 4, CHUNK], F32, ("stage_4k", "stage_8k")[n % 2])
-            d_bank, e_bank = second_products(CHUNK * n + P * b)
-            d_sb = sb(f"d{n}_{b}", [P, 4, P], F32, tag)
-            nc.scalar.copy(d_sb[:].rearrange("p t m -> p (t m)"), d_bank[:])
-            nc.vector.tensor_tensor(
-                y[n][:, :, P * b : P * (b + 1)], e_bank[:].rearrange("p (t m) -> p t m", m=P), d_sb[:], MULT
+        def second_pass(which, bank, col, t, a, c0, width, start, stop):
+            w0 = N * a + P * t
+            cols = slice(c0, c0 + width)
+            codes, scales = (
+                (w4_c[a][:, P * t : P * (t + 1)].bitcast(FP8X4), w4_s),
+                (w5_dw[:, 2 * w0 : 2 * (w0 + P)].bitcast(FP4X4), w5_ds),
+            )[which]
+            nc.tensor.matmul_mx(
+                bank[:, col : col + width], lhsT=codes, lhsT_scale=scales[:, w0 : w0 + P],
+                rhs=z_c[:, cols].bitcast(FP8X4), rhs_scale=z_s[:, cols], start=start, stop=stop,
             )
 
-        def hand_out(n, b0, blocks, mover):
-            part = y[n][:, :, P * b0 : P * (b0 + blocks)]
-            cols = slice(CHUNK * n + P * b0, CHUNK * n + P * (b0 + blocks))
+        def two_banks():
+            return take("mm", mm_banks), take("mm", mm_banks)
+
+        def block_pass(banks, a, c0):
+            for which in range(2):
+                for t in range(4):
+                    second_pass(which, banks[which], P * t, t, a, c0, P, a == 0 and t == 0, a == PASSES - 1 and t == 3)
+
+        def multiply(banks, y_part, name, tag):
+            d_sb = sb(name, [P, BANK], F32, tag)
+            nc.scalar.copy(d_sb[:], banks[0][:])
+            width = y_part.shape[2]
+            nc.vector.tensor_tensor(
+                y_part, banks[1][:].rearrange("p (t m) -> p t m", m=width), d_sb[:].rearrange("p (t m) -> p t m", m=width), MULT
+            )
+
+        def hand_out(part, m0, tag, mover):
+            width = part.shape[2]
+            cols = slice(m0, m0 + width)
             nc.sync.dma_start(y_rows[:, :, cols], part)
-            grouped = sb(f"y_bf{n}_{b0}", [P, 4 * P * blocks], BF16, f"bf{(n + b0) % 2}")
+            grouped = sb(f"y_bf{m0}", [P, 4 * width], BF16, tag)
             interleave(grouped[:], part, mover)
             nc.vector.quantize_mx(y_c[:, cols].bitcast(FP8X4), y_s[:, cols], grouped[:])
 
-        def store_words(n):
-            cols = slice(CHUNK * n, CHUNK * (n + 1))
+        def store_words(m0, width):
+            cols = slice(m0, m0 + width)
             nc.sync.dma_start(y_words[:, cols], y_c[:, cols].bitcast(I32))
 
-        def slots(name, tag):
-            return sb(name, [P, S], F32, tag)
+        def turn_back_first_half(a):
+            for m0 in (0, CHUNK):
+                w0 = S * a + 2 * m0
+                turn_back(a, m0, 2, by_block(z_words[:, w0 : w0 + BANK]), nc.scalar.copy)
 
         gather_table(0)
         quantise_w1(0)
@@ -340,54 +339,91 @@ def tile_list_skat_trick_cubic_kernel(
         first_stage(1, 0)
         finish_values(1, 0)
         quantise_w1(2)
-        for i in range(ROW_TILES):
-            if i + 2 < ROW_TILES:
-                first_stage(i + 2, 0)
-            scatter(i, BANK if i == 0 else S)
-            if i == 1:
+        first_stage(2, 0)
+        finish_values(2, 0)
+        scatter(0, BANK)
+        for half in range(2):
+            sum_picks(0, BANK * half, z_words[:, S * half : S * (half + 1)], last_bank[2])
+        for k in range(ROW_TILES - 1):
+            ahead = k + 3
+            if ahead < ROW_TILES:
+                first_stage(ahead, 0)
+            scatter(k + 1, S)
+            if k == 0:
                 quantise_w1(3)
-            if i in (3, 4):
-                quantise_w4(i - 3)
-            if i + 2 < ROW_TILES:
-                finish_values(i + 2, 0)
-            bank = last_bank[i + 2] if i + 2 < ROW_TILES else take("sum", sum_banks)
-            lead, answer = take("pick", picks)[:], take("pick", picks)[:]
-            sum_picks(i, 0, BANK, lead, answer, bank)
-            if i < 2:
-                sum_picks(i, BANK, BANK, take("pick", picks)[:], take("pick", picks)[:], take("sum", sum_banks))
-            if i % 4 == 3:
-                turn_back(0, i // 4, 0, 2)
-                turn_back(1, i // 4, 0, 2)
+            if k in (2, 3):
+                quantise_w4(k - 2)
+            if ahead < ROW_TILES:
+                finish_values(ahead, 0)
+            bank = last_bank[ahead] if ahead < ROW_TILES else take("sum", sum_banks)
+            if k == 0:
+                sum_picks(1, BANK, b_tiles[1][:], bank)
+            else:
+                sum_picks(k, 0, b_tiles[(k + 1) % 3][:], bank)
+            if k == 3:
+                turn_back_first_half(0)
+        last_picks = b_tiles[ROW_TILES % 3]
+        sum_picks(ROW_TILES - 1, 0, last_picks[:], take("sum", sum_banks))
+        turn_back_first_half(1)
+
         for i in range(2, 6):
-            late_pick(2, i, (lead, answer)[i % 2])
-        quantise_z(0, 0, 2)
-        quantise_z(1, 0, 2)
-        turn_back(2, 0, 0, 2)
-        y_block(0, 0, "a0")
-        y_block(0, 1, "b0")
-        late_picks(2, 6, z_i[1])
-        turn_back(2, 1, 0, 2)
-        late_picks(3, 2, slots("late_b", "a0"))
-        quantise_z(2, 0, 2)
-        hand_out(0, 0, 2, nc.scalar.copy)
-        store_words(0)
-        y_block(1, 0, "c0")
-        y_block(1, 1, "c1")
-        turn_back(3, 0, 0, 2)
-        late_picks(3, 4, slots("late_d", "c0"))
-        hand_out(1, 0, 2, nc.scalar.copy)
-        store_words(1)
-        y_block(2, 0, "b1")
-        late_picks(3, 6, slots("late_e", "c1"))
-        y_block(2, 1, "a1")
+            late_pick(2, i, last_picks[:, BANK * (i % 2) : BANK * (i % 2 + 1)])
+        quantise_z(0, z_words[:])
+        y_half = sb("y_half", [P, 4, BANK], F32, "stage_8k")
+        words2 = z_words[:, S:].rearrange("p (b a m u) -> p b a m u", a=PASSES, m=P, u=2)
+        turn_back(0, 2 * CHUNK, 2, words2[:, :, 0], nc.scalar.copy)
+
+        def half_slice(t, tag):
+            banks = two_banks()
+            for which in range(2):
+                for a in range(PASSES):
+                    second_pass(which, banks[which], 0, t, a, BANK * a, BANK, a == 0, a == PASSES - 1)
+            multiply(banks, y_half[:, t : t + 1, :], f"d_half{t}", tag)
+
+        half_slice(0, "a0")
+        half_slice(1, "a1")
+        late_pick(2, 6, z_words[:, :BANK])
+        late_pick(2, 7, z_words[:, BANK:S])
+        turn_back(1, 2 * CHUNK, 2, words2[:, :, 1], nc.scalar.copy)
+        half_slice(2, "c0")
+        slots = sb("late_a", [P, S], F32, "a1")
+        late_pick(3, 2, slots[:, :BANK])
+        late_pick(3, 3, slots[:, BANK:])
+        half_slice(3, "c1")
+        quantise_z(S, z_words[:, S:])
+        hand_out(y_half[:], 0, "bf0", nc.scalar.copy)
+        store_words(0, BANK)
+        y2 = sb("y2", [P, 4, CHUNK], F32, "stage_4k")
+        banks2 = [two_banks() for b in range(2)]
         for b in range(2):
-            turn_back(3, 1, b, 1)
-            quantise_z(3, b, 1)
-        hand_out(2, 0, 2, nc.scalar.copy)
-        store_words(2)
+            for a in range(PASSES):
+                block_pass(banks2[b], a, S + CHUNK * b + P * a)
+        slots = sb("late_b", [P, S], F32, "c1")
+        late_pick(3, 4, slots[:, :BANK])
+        late_pick(3, 5, slots[:, BANK:])
+        words3 = sb("words3", [P, BANK], F32, "c1")
+        turn_back(0, 3 * CHUNK, 2, by_block(words3[:]), nc.scalar.copy)
+        quantise_z(S + BANK, words3[:])
+        banks3 = []
         for b in range(2):
-            y_block(3, b, ("a0", "b0")[b])
-            hand_out(3, b, 1, nc.vector.tensor_copy)
-        store_words(3)
+            tag = ("b0", "b1")[b]
+            multiply(banks2[b], y2[:, :, P * b : P * (b + 1)], f"d2_{b}", tag)
+            banks3.append(two_banks())
+            block_pass(banks3[b], 0, S + BANK + P * b)
+            slot = sb(f"late_c{b}", [P, BANK], F32, tag)
+            late_pick(3, 6 + b, slot[:])
+        for b in range(2):
+            words = z_words[:, CHUNK * b : CHUNK * (b + 1)]
+            turn_back(1, 3 * CHUNK + P * b, 1, by_block(words), (nc.scalar.copy, nc.vector.tensor_copy)[b])
+            quantise_z(S + BANK + CHUNK + P * b, words)
+        hand_out(y2[:], 2 * CHUNK, "bf1", nc.scalar.copy)
+        store_words(2 * CHUNK, CHUNK)
+        y3 = sb("y3", [P, 4, CHUNK], F32, "v1")
+        for b in range(2):
+            block_pass(banks3[b], 1, S + BANK + CHUNK + P * b)
+            part = y3[:, :, P * b : P * (b + 1)]
+            multiply(banks3[b], part, f"d3_{b}", ("a0", "c0")[b])
+            hand_out(part, 3 * CHUNK + P * b, ("bf0", "bf1")[b], nc.vector.tensor_copy)
+        store_words(3 * CHUNK, CHUNK)
         for q in range(4):
             (nc.sync, nc.scalar)[q % 2].dma_start(out_2[0, 4 * q : 4 * q + 4, :].bitcast(I32), y_s[32 * q : 32 * q + 4, :].bitcast(I32))

@@ -15,6 +15,7 @@ U8 = mybir.dt.uint8
 FP8X4 = mybir.dt.float8_e4m3fn_x4
 FP4X4 = mybir.dt.float4_e2m1fn_x4
 MULT = mybir.AluOpType.mult
+ADD = mybir.AluOpType.add
 
 P = 128
 BANK = 512
@@ -22,7 +23,6 @@ ROW_TILES = H // P
 PASSES = H // 512
 W1_CHUNKS = ((0, 128), (128, 128), (256, 256), (512, 512))
 CHUNK = 256
-CHUNKS = M // CHUNK
 
 
 def tile_list_skat_trick_cubic_kernel(
@@ -54,7 +54,7 @@ def tile_list_skat_trick_cubic_kernel(
         mm_banks = [psum.tile([P, BANK], F32, name=f"mm_bank{b}") for b in range(4)]
         sum_banks = [psum.tile([P, BANK], F32, name=f"sum_bank{b}") for b in range(2)]
         back_banks = [psum.tile([P, BANK], F32, name=f"back_bank{b}") for b in range(2)]
-        turns = {"mm": 0, "sum": 0, "back": 0, "pick": 0, "late": 0}
+        turns = {"mm": 0, "sum": 0, "back": 0}
 
         def take(kind, tiles):
             tile = tiles[turns[kind] % len(tiles)]
@@ -163,19 +163,6 @@ def tile_list_skat_trick_cubic_kernel(
             w4_c[a] = sb(f"w4_c{a}", [P, N], U32)
             nc.vector.quantize_mx(w4_c[a][:].bitcast(FP8X4), w4_s[:, cols], grouped[:])
 
-        w5_dw = sb("w5_dw", [P, PASSES * 2 * N], U8)
-        w5_ds = sb("w5_ds", [P, PASSES * N], U8)
-
-        def deal_w5():
-            nc.vector.tensor_copy(
-                w5_dw[:].bitcast(U16).rearrange("p (a t m) -> p a t m", a=PASSES, t=4),
-                w5_w[:].bitcast(U16).rearrange("p (a m t) -> p a t m", a=PASSES, t=4),
-            )
-            nc.vector.tensor_copy(
-                w5_ds[:].rearrange("p (a t m) -> p a t m", a=PASSES, t=4),
-                w5_s[:].rearrange("p (a m t) -> p a t m", a=PASSES, t=4),
-            )
-
         a_tiles = [sb(f"a{n}", [P, S], F32) for n in range(2)]
         b_tiles = [sb(f"b{n}", [P, S], F32) for n in range(3)]
         c_tiles = [sb(f"c{n}", [P, S], F32) for n in range(2)]
@@ -278,6 +265,22 @@ def tile_list_skat_trick_cubic_kernel(
             cols = slice(c0, c0 + words.shape[1] // 2)
             nc.vector.quantize_mx(z_c[:, cols].bitcast(FP8X4), z_s[:, cols], words.bitcast(BF16))
 
+        w5_dealt = {}
+
+        def deal_w5():
+            words = sb("w5_dw", [P, PASSES * 2 * N], U8, "a1")
+            scales = sb("w5_ds", [P, PASSES * N], U8, "c1")
+            nc.gpsimd.tensor_copy(
+                words[:].rearrange("p (a t m b) -> p a t m b", a=PASSES, t=4, b=2),
+                w5_w[:].rearrange("p (a m t b) -> p a t m b", a=PASSES, t=4, b=2),
+            )
+            nc.gpsimd.tensor_copy(
+                scales[:].rearrange("p (a t m) -> p a t m", a=PASSES, t=4),
+                w5_s[:].rearrange("p (a m t) -> p a t m", a=PASSES, t=4),
+            )
+            w5_dealt["words"] = words
+            w5_dealt["scales"] = scales
+
         y_c = sb("y_c", [P, M], U32)
         y_s = sb("y_s", [P, M], U8)
         y_rows = out_0.rearrange("(p t) m -> p t m", t=4)
@@ -288,7 +291,7 @@ def tile_list_skat_trick_cubic_kernel(
             cols = slice(c0, c0 + width)
             codes, scales = (
                 (w4_c[a][:, P * t : P * (t + 1)].bitcast(FP8X4), w4_s),
-                (w5_dw[:, 2 * w0 : 2 * (w0 + P)].bitcast(FP4X4), w5_ds),
+                (w5_dealt["words"][:, 2 * w0 : 2 * (w0 + P)].bitcast(FP4X4), w5_dealt["scales"]),
             )[which]
             nc.tensor.matmul_mx(
                 bank[:, col : col + width], lhsT=codes, lhsT_scale=scales[:, w0 : w0 + P],
@@ -311,12 +314,20 @@ def tile_list_skat_trick_cubic_kernel(
                 y_part, banks[1][:].rearrange("p (t m) -> p t m", m=width), d_sb[:].rearrange("p (t m) -> p t m", m=width), MULT
             )
 
-        def hand_out(part, m0, tag, mover):
+        def round_on_gpsimd(dst, src):
+            nc.gpsimd.tensor_scalar(
+                dst.rearrange("p (m t) -> p m t", t=4), src.rearrange("p t m -> p m t"), 1.0, 0.0, MULT, ADD
+            )
+
+        def round_on_vector(dst, src):
+            interleave(dst, src, nc.vector.tensor_copy)
+
+        def hand_out(part, m0, tag, rounder):
             width = part.shape[2]
             cols = slice(m0, m0 + width)
             nc.sync.dma_start(y_rows[:, :, cols], part)
             grouped = sb(f"y_bf{m0}", [P, 4 * width], BF16, tag)
-            interleave(grouped[:], part, mover)
+            rounder(grouped[:], part)
             nc.vector.quantize_mx(y_c[:, cols].bitcast(FP8X4), y_s[:, cols], grouped[:])
 
         def store_words(m0, width):
@@ -335,7 +346,6 @@ def tile_list_skat_trick_cubic_kernel(
         first_stage(0, BANK)
         finish_values(0, BANK)
         quantise_w1(1)
-        deal_w5()
         first_stage(1, 0)
         finish_values(1, 0)
         quantise_w1(2)
@@ -365,12 +375,14 @@ def tile_list_skat_trick_cubic_kernel(
         last_picks = b_tiles[ROW_TILES % 3]
         sum_picks(ROW_TILES - 1, 0, last_picks[:], take("sum", sum_banks))
         turn_back_first_half(1)
+        deal_w5()
 
         for i in range(2, 6):
             late_pick(2, i, last_picks[:, BANK * (i % 2) : BANK * (i % 2 + 1)])
         quantise_z(0, z_words[:])
         y_half = sb("y_half", [P, 4, BANK], F32, "stage_8k")
-        words2 = z_words[:, S:].rearrange("p (b a m u) -> p b a m u", a=PASSES, m=P, u=2)
+        words2_flat = sb("words2", [P, S], F32, "w4_raw0")
+        words2 = words2_flat[:].rearrange("p (b a m u) -> p b a m u", a=PASSES, m=P, u=2)
         turn_back(0, 2 * CHUNK, 2, words2[:, :, 0], nc.scalar.copy)
 
         def half_slice(t, tag):
@@ -378,52 +390,53 @@ def tile_list_skat_trick_cubic_kernel(
             for which in range(2):
                 for a in range(PASSES):
                     second_pass(which, banks[which], 0, t, a, BANK * a, BANK, a == 0, a == PASSES - 1)
-            multiply(banks, y_half[:, t : t + 1, :], f"d_half{t}", tag)
+            both = sb(f"de_half{t}", [P, S], F32, tag)
+            for which in range(2):
+                nc.scalar.copy(both[:, BANK * which : BANK * (which + 1)], banks[which][:])
+            nc.gpsimd.tensor_tensor(y_half[:, t, :], both[:, :BANK], both[:, BANK:], MULT)
 
+        quarters = [z_words[:, j : j + BANK] for j in range(0, 2 * S, BANK)]
         half_slice(0, "a0")
-        half_slice(1, "a1")
-        late_pick(2, 6, z_words[:, :BANK])
-        late_pick(2, 7, z_words[:, BANK:S])
+        half_slice(1, "c0")
+        half_slice(2, "v1")
+        late_pick(2, 6, quarters[0])
+        late_pick(2, 7, quarters[1])
         turn_back(1, 2 * CHUNK, 2, words2[:, :, 1], nc.scalar.copy)
-        half_slice(2, "c0")
-        slots = sb("late_a", [P, S], F32, "a1")
-        late_pick(3, 2, slots[:, :BANK])
-        late_pick(3, 3, slots[:, BANK:])
-        half_slice(3, "c1")
-        quantise_z(S, z_words[:, S:])
-        hand_out(y_half[:], 0, "bf0", nc.scalar.copy)
-        store_words(0, BANK)
+        half_slice(3, "b0")
+        late_pick(3, 2, quarters[2])
+        late_pick(3, 3, quarters[3])
+        words3 = sb("words3", [P, BANK], F32, "b2")
+        turn_back(0, 3 * CHUNK, 2, by_block(words3[:]), nc.scalar.copy)
+        late_pick(3, 4, quarters[0])
+        quantise_z(S, words2_flat[:])
+        quantise_z(S + BANK, words3[:])
         y2 = sb("y2", [P, 4, CHUNK], F32, "stage_4k")
         banks2 = [two_banks() for b in range(2)]
         for b in range(2):
             for a in range(PASSES):
                 block_pass(banks2[b], a, S + CHUNK * b + P * a)
-        slots = sb("late_b", [P, S], F32, "c1")
-        late_pick(3, 4, slots[:, :BANK])
-        late_pick(3, 5, slots[:, BANK:])
-        words3 = sb("words3", [P, BANK], F32, "c1")
-        turn_back(0, 3 * CHUNK, 2, by_block(words3[:]), nc.scalar.copy)
-        quantise_z(S + BANK, words3[:])
-        banks3 = []
+        late_pick(3, 5, words2_flat[:, :BANK])
+        late_pick(3, 6, words2_flat[:, BANK:])
+        late_pick(3, 7, words3[:])
         for b in range(2):
-            tag = ("b0", "b1")[b]
-            multiply(banks2[b], y2[:, :, P * b : P * (b + 1)], f"d2_{b}", tag)
-            banks3.append(two_banks())
-            block_pass(banks3[b], 0, S + BANK + P * b)
-            slot = sb(f"late_c{b}", [P, BANK], F32, tag)
-            late_pick(3, 6 + b, slot[:])
+            multiply(banks2[b], y2[:, :, P * b : P * (b + 1)], f"d2_{b}", ("b1", "a0")[b])
         for b in range(2):
-            words = z_words[:, CHUNK * b : CHUNK * (b + 1)]
+            words = quarters[1][:, CHUNK * b : CHUNK * (b + 1)]
             turn_back(1, 3 * CHUNK + P * b, 1, by_block(words), (nc.scalar.copy, nc.vector.tensor_copy)[b])
             quantise_z(S + BANK + CHUNK + P * b, words)
-        hand_out(y2[:], 2 * CHUNK, "bf1", nc.scalar.copy)
+        banks3 = [two_banks() for b in range(2)]
+        for b in range(2):
+            block_pass(banks3[b], 0, S + BANK + P * b)
+        hand_out(y_half[:], 0, "bf0", round_on_gpsimd)
+        store_words(0, BANK)
+        hand_out(y2[:], 2 * CHUNK, "bf1", round_on_vector)
         store_words(2 * CHUNK, CHUNK)
-        y3 = sb("y3", [P, 4, CHUNK], F32, "v1")
+        y3 = sb("y3", [P, 4, CHUNK], F32, "w4_raw1")
         for b in range(2):
             block_pass(banks3[b], 1, S + BANK + CHUNK + P * b)
             part = y3[:, :, P * b : P * (b + 1)]
-            multiply(banks3[b], part, f"d3_{b}", ("a0", "c0")[b])
-            hand_out(part, 3 * CHUNK + P * b, ("bf0", "bf1")[b], nc.vector.tensor_copy)
+            multiply(banks3[b], part, f"d3_{b}", ("c0", "v1")[b])
+            hand_out(part, 3 * CHUNK + P * b, ("bf0", "bf1")[b], round_on_vector)
         store_words(3 * CHUNK, CHUNK)
         for q in range(4):
             (nc.sync, nc.scalar)[q % 2].dma_start(out_2[0, 4 * q : 4 * q + 4, :].bitcast(I32), y_s[32 * q : 32 * q + 4, :].bitcast(I32))

from contextlib import ExitStack

import concourse.mybir as mybir
from concourse.masks import make_identity

K, T, H, S, T2, M, N = 512, 2048, 1024, 1024, 2048, 1024, 512
FLOPS = 2 * (3 * K * H * S + 2 * H * N * M)

F32 = mybir.dt.float32
BF16 = mybir.dt.bfloat16
I32 = mybir.dt.int32
U32 = mybir.dt.uint32
U16 = mybir.dt.uint16
U8 = mybir.dt.uint8
FP8X4 = mybir.dt.float8_e4m3fn_x4
FP4X4 = mybir.dt.float4_e2m1fn_x4
MULT = mybir.AluOpType.mult
ADD = mybir.AluOpType.add

P = 128
BANK = 512
ROW_TILES = H // P
PASSES = H // 512
W1_CHUNKS = ((0, 128), (128, 128), (256, 256), (512, 512))
CHUNK = 256


def tile_list_skat_trick_cubic_kernel(
    tc, tab_words, tab_scales, offs, w1, w2_words, w2_scales, w3_words, w3_scales,
    page0, wgs, offs2, offs3, offs4, w4, w5_words, w5_scales, out_0, out_1, out_2,
):
    nc = tc.nc
    with ExitStack() as ctx:
        lists = ctx.enter_context(tc.tile_pool(name="lists", bufs=1))
        keep = ctx.enter_context(tc.tile_pool(name="keep", bufs=1))
        psum = ctx.enter_context(tc.psum_pool(name="psum", bufs=1))

        def sb(name, shape, dtype, tag=None):
            return keep.tile(shape, dtype, name=name, tag=tag or name, align_bytes=64)

        def load_list(name, src):
            tile = lists.tile([P, 64], U16, name=name)
            nc.sync.dma_start(tile[:], src)
            return tile

        def load_plane(plane, scales, queue):
            passes = scales.shape[0]
            for q in range(4):
                queue.dma_start(
                    plane[32 * q : 32 * q + 4, :].bitcast(I32).rearrange("r (a c) -> r a c", a=passes),
                    scales[:, 4 * q : 4 * q + 4, :].bitcast(I32).rearrange("a r c -> r a c"),
                )

        mm_banks = [psum.tile([P, BANK], F32, name=f"mm_bank{b}") for b in range(4)]
        sum_banks = [psum.tile([P, BANK], F32, name=f"sum_bank{b}") for b in range(2)]
        back_banks = [psum.tile([P, BANK], F32, name=f"back_bank{b}") for b in range(2)]
        turns = {"mm": 0, "sum": 0, "back": 0}

        def take(kind, tiles):
            tile = tiles[turns[kind] % len(tiles)]
            turns[kind] = turns[kind] + 1
            return tile

        tab_w = sb("tab_w", [P, T], U32)
        tab_s = sb("tab_s", [P, T], U8)
        w2_w = sb("w2_w", [P, 2 * H], U8)
        w2_s = sb("w2_s", [P, H], U8)
        w3_w = sb("w3_w", [P, H], U32)
        w3_s = sb("w3_s", [P, H], U8)
        w5_w = sb("w5_w", [P, PASSES * 2 * N], U8)
        w5_s = sb("w5_s", [P, PASSES * N], U8)
        for plane in (tab_s, w3_s, w5_s):
            nc.vector.memset(plane[:].bitcast(I32), 0)
        nc.gpsimd.memset(w2_s[:].bitcast(I32), 0)
        load_plane(w2_s, w2_scales, nc.gpsimd)
        ident = sb("ident", [P, P], F32)
        make_identity(nc, ident[:])

        w1_rows = w1.rearrange("(p j) c -> p j c", j=4)
        w1_tags = ("w1_raw0", "w1_raw1", "stage_4k", "stage_8k")
        w1_raw = [sb(f"w1_raw{n}", [P, 4, width], F32, w1_tags[n]) for n, (c0, width) in enumerate(W1_CHUNKS)]

        def load_w1(n):
            c0, width = W1_CHUNKS[n]
            nc.sync.dma_start(w1_raw[n][:], w1_rows[:, :, c0 : c0 + width])

        pages = [sb(f"page{i}", [P, T2], F32) for i in range(ROW_TILES)]

        def load_page(i):
            nc.sync.dma_start(pages[i][:], page0[P * i : P * (i + 1), :])

        idx = load_list("idx", offs)
        nc.sync.dma_start(tab_w[:].bitcast(I32), tab_words[0].rearrange("p t i -> p (t i)").bitcast(I32))
        load_plane(tab_s, tab_scales, nc.sync)
        load_w1(0)
        w2_src = w2_words[0].bitcast(I32)
        w3_src = w3_words[0].rearrange("p c i -> p (c i)").bitcast(I32)
        nc.sync.dma_start(w2_w[:, : 2 * P].bitcast(I32), w2_src[:, : P // 2])
        nc.sync.dma_start(w3_w[:, :P].bitcast(I32), w3_src[:, :P])
        idx2 = load_list("idx2", offs2)
        idx3 = load_list("idx3", offs3)
        idx4 = load_list("idx4", offs4)
        load_plane(w3_s, w3_scales, nc.sync)
        wgs_sb = sb("wgs_sb", [P, S], F32)
        nc.sync.dma_start(wgs_sb[:], wgs)
        load_w1(1)
        nc.sync.dma_start(w2_w[:, 2 * P :].bitcast(I32), w2_src[:, P // 2 :])
        nc.sync.dma_start(w3_w[:, P:].bitcast(I32), w3_src[:, P:])
        load_page(0)
        load_w1(2)
        load_plane(w5_s, w5_scales, nc.sync)
        nc.sync.dma_start(
            w5_w[:].bitcast(I32).rearrange("p (a c) -> p a c", a=PASSES),
            w5_words.bitcast(I32).rearrange("a p c -> p a c"),
        )
        load_page(1)
        load_w1(3)
        load_page(2)
        w4_rows = w4.rearrange("(a p j) n -> a p j n", a=PASSES, j=4)
        w4_raw = [sb(f"w4_raw{a}", [P, 4, N], F32) for a in range(PASSES)]
        for a in range(PASSES):
            nc.sync.dma_start(w4_raw[a][:], w4_rows[a])
        for i in range(3, ROW_TILES):
            load_page(i)

        v_w = sb("v_w", [P, S], U32)
        v_s = sb("v_s", [P, S], U8)

        def gather_table(half):
            cols = slice(BANK * half, BANK * (half + 1))
            entries = idx[:, 32 * half : 32 * (half + 1)]
            nc.vector.tensor_copy(v_w[:, cols], tab_w[:].indirect(entries))
            nc.vector.tensor_copy(v_s[:, cols], tab_s[:].indirect(entries))

        w1_c = {}
        w1_s = sb("w1_s", [P, H], U8)

        def interleave(dst, src, mover):
            mover(
                dst.rearrange("p (c i t) -> p c t i", i=4, t=4),
                src.rearrange("p t (c i) -> p c t i", i=4),
            )

        def quantise_w1(n):
            c0, width = W1_CHUNKS[n]
            grouped = sb(f"w1_bf{n}", [P, 4 * width], BF16, f"bf{n % 2}")
            interleave(grouped[:], w1_raw[n][:], nc.scalar.copy)
            codes = sb(f"w1_c{n}", [P, width], U32)
            nc.vector.quantize_mx(codes[:].bitcast(FP8X4), w1_s[:, c0 : c0 + width], grouped[:])
            for c in range(0, width, P):
                w1_c[(c0 + c) // P] = codes[:, c : c + P]

        w4_c = {}
        w4_s = sb("w4_s", [P, PASSES * N], U8)

        def quantise_w4(a):
            grouped = sb(f"w4_bf{a}", [P, 4 * N], BF16, "bf0")
            nc.scalar.copy(
                grouped[:].rearrange("p (t m j) -> p m t j", t=4, j=4),
                w4_raw[a][:].rearrange("p j (m t) -> p m t j", t=4),
            )
            cols = slice(N * a, N * (a + 1))
            w4_c[a] = sb(f"w4_c{a}", [P, N], U32)
            nc.vector.quantize_mx(w4_c[a][:].bitcast(FP8X4), w4_s[:, cols], grouped[:])

        a_tiles = [sb(f"a{n}", [P, S], F32) for n in range(2)]
        b_tiles = [sb(f"b{n}", [P, S], F32) for n in range(3)]
        c_tiles = [sb(f"c{n}", [P, S], F32) for n in range(2)]
        value_tags = ("v0", "w1_c3", "v1", "w4_c0", "w4_c1", "v0", "v1", "v0")
        values = {}
        last_bank = {}

        def abc(i):
            return a_tiles[i % 2], b_tiles[i % 3], c_tiles[i % 2]

        def value_tile(i):
            if i not in values:
                values[i] = sb(f"values{i}", [P, S], F32, value_tags[i])
            return values[i]

        def product(i, which, j):
            rows = slice(P * i, P * (i + 1))
            codes, scales = (
                (w1_c[i].bitcast(FP8X4), w1_s[:, rows]),
                (w2_w[:, 2 * P * i : 2 * P * (i + 1)].bitcast(FP4X4), w2_s[:, rows]),
                (w3_w[:, rows].bitcast(FP8X4), w3_s[:, rows]),
            )[which]
            cols = slice(j, j + BANK)
            bank = take("mm", mm_banks)
            nc.tensor.matmul_mx(
                bank[:], lhsT=codes, lhsT_scale=scales,
                rhs=v_w[:, cols].bitcast(FP8X4), rhs_scale=v_s[:, cols], start=True, stop=True,
            )
            last_bank[i] = bank
            return bank

        def first_values_on_vector():
            a_sb, b_sb, c_sb = abc(0)
            cols = slice(0, BANK)
            nc.scalar.copy(a_sb[:, cols], product(0, 0, 0)[:])
            nc.vector.tensor_tensor(c_sb[:, cols], product(0, 2, 0)[:], wgs_sb[:, cols], MULT)
            nc.vector.tensor_tensor(b_sb[:, cols], product(0, 1, 0)[:], a_sb[:, cols], MULT)
            nc.vector.tensor_tensor(value_tile(0)[:, cols], b_sb[:, cols], c_sb[:, cols], MULT)

        def first_stage(i, j0):
            a_sb, b_sb, c_sb = abc(i)
            for which in (1, 2, 0):
                for j in range(j0, S, BANK):
                    nc.scalar.copy(abc(i)[which][:, j : j + BANK], product(i, which, j)[:])
            nc.gpsimd.tensor_tensor(b_sb[:, j0:], b_sb[:, j0:], c_sb[:, j0:], MULT)
            nc.gpsimd.tensor_tensor(a_sb[:, j0:], a_sb[:, j0:], wgs_sb[:, j0:], MULT)

        def finish_values(i, j0):
            a_sb, b_sb, c_sb = abc(i)
            nc.gpsimd.tensor_tensor(value_tile(i)[:, j0:], a_sb[:, j0:], b_sb[:, j0:], MULT)

        def scatter(i, step):
            for j0 in range(0, S, step):
                entries = idx2[:, j0 // 16 : (j0 + step) // 16]
                nc.vector.tensor_copy(pages[i][:].indirect(entries), values[i][:, j0 : j0 + step])

        z_t = [[sb(f"z_t{a}_{half}", [P, 4, 2, P, 2], BF16) for half in range(2)] for a in range(PASSES)]

        def sum_picks(i, m0, slot, bank):
            width = slot.shape[1] // 2
            lead, answer = slot[:, :width], slot[:, width:]
            entries = slice(m0 // 16, (m0 + width) // 16)
            nc.vector.tensor_copy(lead, pages[i][:].indirect(idx3[:, entries]))
            nc.vector.tensor_copy(answer, pages[i][:].indirect(idx4[:, entries]))
            for m in range(0, width, P):
                cols = slice(m, m + P)
                nc.tensor.matmul(bank[:, cols], lead[:, cols], ident[:], start=(m == 0), stop=False, is_transpose=True)
            for m in range(0, width, P):
                cols = slice(m, m + P)
                nc.tensor.matmul(
                    bank[:, cols], answer[:, cols], ident[:], start=False, stop=(m + P == width), is_transpose=True
                )
            q = i % 4
            b0 = m0 // P % 4
            nc.scalar.copy(
                z_t[i // 4][m0 // BANK][:, b0 : b0 + width // P, :, 32 * q : 32 * (q + 1), :],
                bank[:, :width].rearrange("m (b p u e) -> m b u p e", p=32, u=2, e=2),
            )

        def late_pick(n, i, slot):
            sum_picks(i, CHUNK * n, slot, take("sum", sum_banks))

        def turn_back(a, m0, blocks, words, mover):
            bank = take("back", back_banks)
            for b in range(blocks):
                for u in range(2):
                    col = P * (2 * b + u)
                    src = z_t[a][m0 // BANK][:, m0 // P % 4 + b, u].rearrange("m p e -> m (p e)").bitcast(F32)
                    nc.tensor.transpose(bank[:, col : col + P], src, ident[:])
            mover(words, bank[:, : 2 * P * blocks].rearrange("p (b u m) -> p b m u", u=2, m=P))

        def by_block(words):
            return words.rearrange("p (b m u) -> p b m u", m=P, u=2)

        z_words = sb("z_words", [P, 2 * S], F32)
        z_c = sb("z_c", [P, PASSES * M], U32)
        z_s = sb("z_s", [P, PASSES * M], U8)

        def quantise_z(c0, words):
            cols = slice(c0, c0 + words.shape[1] // 2)
            nc.vector.quantize_mx(z_c[:, cols].bitcast(FP8X4), z_s[:, cols], words.bitcast(BF16))

        w5_dealt = {}

        def deal_w5():
            words = sb("w5_dw", [P, PASSES * 2 * N], U8, "a1")
            scales = sb("w5_ds", [P, PASSES * N], U8, "c1")
            nc.gpsimd.tensor_copy(
                words[:].rearrange("p (a t m b) -> p a t m b", a=PASSES, t=4, b=2),
                w5_w[:].rearrange("p (a m t b) -> p a t m b", a=PASSES, t=4, b=2),
            )
            nc.gpsimd.tensor_copy(
                scales[:].rearrange("p (a t m) -> p a t m", a=PASSES, t=4),
                w5_s[:].rearrange("p (a m t) -> p a t m", a=PASSES, t=4),
            )
            w5_dealt["words"] = words
            w5_dealt["scales"] = scales

        y_c = sb("y_c", [P, M], U32)
        y_s = sb("y_s", [P, M], U8)
        y_rows = out_0.rearrange("(p t) m -> p t m", t=4)
        y_words = out_1[0].rearrange("p m t -> p (m t)").bitcast(I32)

        def second_pass(which, bank, col, t, a, c0, width, start, stop):
            w0 = N * a + P * t
            cols = slice(c0, c0 + width)
            codes, scales = (
                (w4_c[a][:, P * t : P * (t + 1)].bitcast(FP8X4), w4_s),
                (w5_dealt["words"][:, 2 * w0 : 2 * (w0 + P)].bitcast(FP4X4), w5_dealt["scales"]),
            )[which]
            nc.tensor.matmul_mx(
                bank[:, col : col + width], lhsT=codes, lhsT_scale=scales[:, w0 : w0 + P],
                rhs=z_c[:, cols].bitcast(FP8X4), rhs_scale=z_s[:, cols], start=start, stop=stop,
            )

        def two_banks():
            return take("mm", mm_banks), take("mm", mm_banks)

        def block_pass(banks, a, c0):
            for which in range(2):
                for t in range(4):
                    second_pass(which, banks[which], P * t, t, a, c0, P, a == 0 and t == 0, a == PASSES - 1 and t == 3)

        def multiply(banks, y_part, name, tag):
            d_sb = sb(name, [P, BANK], F32, tag)
            nc.scalar.copy(d_sb[:], banks[0][:])
            width = y_part.shape[2]
            nc.vector.tensor_tensor(
                y_part, banks[1][:].rearrange("p (t m) -> p t m", m=width), d_sb[:].rearrange("p (t m) -> p t m", m=width), MULT
            )

        def round_on_gpsimd(dst, src):
            nc.gpsimd.tensor_scalar(
                dst.rearrange("p (m t) -> p m t", t=4), src.rearrange("p t m -> p m t"), 1.0, 0.0, MULT, ADD
            )

        def round_on_vector(dst, src):
            interleave(dst, src, nc.vector.tensor_copy)

        def hand_out(part, m0, tag, rounder):
            width = part.shape[2]
            cols = slice(m0, m0 + width)
            nc.sync.dma_start(y_rows[:, :, cols], part)
            grouped = sb(f"y_bf{m0}", [P, 4 * width], BF16, tag)
            rounder(grouped[:], part)
            nc.vector.quantize_mx(y_c[:, cols].bitcast(FP8X4), y_s[:, cols], grouped[:])

        def store_words(m0, width):
            cols = slice(m0, m0 + width)
            nc.sync.dma_start(y_words[:, cols], y_c[:, cols].bitcast(I32))

        def turn_back_first_half(a):
            for m0 in (0, CHUNK):
                w0 = S * a + 2 * m0
                turn_back(a, m0, 2, by_block(z_words[:, w0 : w0 + BANK]), nc.scalar.copy)

        gather_table(0)
        quantise_w1(0)
        gather_table(1)
        first_values_on_vector()
        first_stage(0, BANK)
        finish_values(0, BANK)
        quantise_w1(1)
        first_stage(1, 0)
        finish_values(1, 0)
        quantise_w1(2)
        first_stage(2, 0)
        finish_values(2, 0)
        scatter(0, BANK)
        for half in range(2):
            sum_picks(0, BANK * half, z_words[:, S * half : S * (half + 1)], last_bank[2])
        for k in range(ROW_TILES - 1):
            ahead = k + 3
            if ahead < ROW_TILES:
                first_stage(ahead, 0)
            scatter(k + 1, S)
            if k == 0:
                quantise_w1(3)
            if k in (2, 3):
                quantise_w4(k - 2)
            if ahead < ROW_TILES:
                finish_values(ahead, 0)
            bank = last_bank[ahead] if ahead < ROW_TILES else take("sum", sum_banks)
            if k == 0:
                sum_picks(1, BANK, b_tiles[1][:], bank)
            else:
                sum_picks(k, 0, b_tiles[(k + 1) % 3][:], bank)
            if k == 3:
                turn_back_first_half(0)
        last_picks = b_tiles[ROW_TILES % 3]
        sum_picks(ROW_TILES - 1, 0, last_picks[:], take("sum", sum_banks))
        turn_back_first_half(1)
        deal_w5()

        for i in range(2, 6):
            late_pick(2, i, last_picks[:, BANK * (i % 2) : BANK * (i % 2 + 1)])
        quantise_z(0, z_words[:])
        y_half = sb("y_half", [P, 4, BANK], F32, "stage_8k")
        words2_flat = sb("words2", [P, S], F32, "w4_raw0")
        words2 = words2_flat[:].rearrange("p (b a m u) -> p b a m u", a=PASSES, m=P, u=2)
        turn_back(0, 2 * CHUNK, 2, words2[:, :, 0], nc.scalar.copy)

        def half_slice(t, tag):
            banks = two_banks()
            for which in range(2):
                for a in range(PASSES):
                    second_pass(which, banks[which], 0, t, a, BANK * a, BANK, a == 0, a == PASSES - 1)
            both = sb(f"de_half{t}", [P, S], F32, tag)
            for which in range(2):
                nc.scalar.copy(both[:, BANK * which : BANK * (which + 1)], banks[which][:])
            nc.gpsimd.tensor_tensor(y_half[:, t, :], both[:, :BANK], both[:, BANK:], MULT)

        quarters = [z_words[:, j : j + BANK] for j in range(0, 2 * S, BANK)]
        half_slice(0, "a0")
        half_slice(1, "c0")
        half_slice(2, "v1")
        late_pick(2, 6, quarters[0])
        late_pick(2, 7, quarters[1])
        turn_back(1, 2 * CHUNK, 2, words2[:, :, 1], nc.scalar.copy)
        half_slice(3, "b0")
        late_pick(3, 2, quarters[2])
        late_pick(3, 3, quarters[3])
        words3 = sb("words3", [P, BANK], F32, "b2")
        turn_back(0, 3 * CHUNK, 2, by_block(words3[:]), nc.scalar.copy)
        late_pick(3, 4, quarters[0])
        quantise_z(S, words2_flat[:])
        quantise_z(S + BANK, words3[:])
        y2 = sb("y2", [P, 4, CHUNK], F32, "stage_4k")
        banks2 = [two_banks() for b in range(2)]
        for b in range(2):
            for a in range(PASSES):
                block_pass(banks2[b], a, S + CHUNK * b + P * a)
        late_pick(3, 5, words2_flat[:, :BANK])
        late_pick(3, 6, words2_flat[:, BANK:])
        late_pick(3, 7, words3[:])
        for b in range(2):
            multiply(banks2[b], y2[:, :, P * b : P * (b + 1)], f"d2_{b}", ("b1", "a0")[b])
        for b in range(2):
            words = quarters[1][:, CHUNK * b : CHUNK * (b + 1)]
            turn_back(1, 3 * CHUNK + P * b, 1, by_block(words), (nc.scalar.copy, nc.vector.tensor_copy)[b])
            quantise_z(S + BANK + CHUNK + P * b, words)
        banks3 = [two_banks() for b in range(2)]
        for b in range(2):
            block_pass(banks3[b], 0, S + BANK + P * b)
        hand_out(y_half[:], 0, "bf0", round_on_gpsimd)
        store_words(0, BANK)
        hand_out(y2[:], 2 * CHUNK, "bf1", round_on_vector)
        store_words(2 * CHUNK, CHUNK)
        y3 = sb("y3", [P, 4, CHUNK], F32, "w4_raw1")
        for b in range(2):
            block_pass(banks3[b], 1, S + BANK + CHUNK + P * b)
            part = y3[:, :, P * b : P * (b + 1)]
            multiply(banks3[b], part, f"d3_{b}", ("c0", "v1")[b])
            hand_out(part, 3 * CHUNK + P * b, ("bf0", "bf1")[b], round_on_vector)
        store_words(3 * CHUNK, CHUNK)
        for q in range(4):
            (nc.sync, nc.scalar)[q % 2].dma_start(out_2[0, 4 * q : 4 * q + 4, :].bitcast(I32), y_s[32 * q : 32 * q + 4, :].bitcast(I32))
